import numpy as np
import ml_dtypes


def mxq(x, axis, fmt="e4m3"):
    dtype, down = {"e4m3": (ml_dtypes.float8_e4m3fn, 7), "e5m2": (ml_dtypes.float8_e5m2, 14)}[fmt]
    v = np.moveaxis(np.asarray(x, np.float32).astype(ml_dtypes.bfloat16).astype(np.float64), axis, -1)
    blocks = v.reshape(v.shape[:-1] + (-1, 32))
    amax = np.abs(blocks).max(-1, keepdims=True)
    byte = np.maximum(np.where(amax > 0, np.frexp(amax)[1] - 1 + 127, 0) - down, 1)
    scale = np.exp2(byte - 127.0)
    codes = (blocks / scale).astype(np.float32).astype(dtype).astype(np.float64)
    return np.moveaxis((codes * scale).reshape(v.shape), -1, axis)


WIDE = False


def mx_kscale(k):
    if not WIDE:
        return np.ones(k)
    levels = np.array([18, -18])
    if k % 512:
        return np.exp2(np.random.permutation(np.resize(levels, k // 32))).repeat(32)
    a = np.empty((k // 512, 16))
    for p in range(k // 512):
        a[p, :8] = np.random.permutation(np.resize(levels, 8))
        for g in range(8):
            far = levels[np.abs(levels - a[p, g]) >= 10]
            a[p, g + 8] = far[np.random.randint(len(far))]
    return np.exp2(a.ravel()).repeat(32)


def f64(x):
    return np.asarray(x).astype(np.float64)


def striped(idx):
    return np.tile(np.asarray(idx).reshape(-1, 16).T, (8, 1)).astype(np.uint16)


def unstriped(offs):
    return offs[:16].T.reshape(-1).astype(np.int64)

def planes(y):
    n, m = y.shape
    v = y.astype(np.float32).astype(ml_dtypes.bfloat16).astype(np.float64).reshape(n // 32, 32, m)
    top = np.abs(v).max(1)
    byte = np.clip(np.where(top > 0, np.frexp(top)[1] - 1 + 127 - 7, 1), 1, 254)
    codes = (v * np.exp2(127.0 - byte)[:, None, :]).reshape(n, m).astype(np.float32).astype(ml_dtypes.float8_e4m3fn).view(np.uint8)
    words = codes.reshape(n // 512, 128, 4, m).transpose(0, 1, 3, 2)
    return np.ascontiguousarray(words), np.ascontiguousarray(byte.astype(np.uint8).reshape(n // 512, 16, m))


B, N, T, D, DV, R = 1, 512, 2048, 512, 512, 1024
PAGE = 64


def setup_inputs():
    n = np.random.standard_normal
    pages = np.random.permutation(T // PAGE)[:B * N // PAGE]
    idx = (pages[:, None] * PAGE + np.arange(PAGE)[None, :]).reshape(-1)
    s = mx_kscale(D)[:, None]
    z = mx_kscale(R)[:, None]
    v = mx_kscale(DV)[:, None]
    q = n((B, D, R))
    do = n((B, DV, R))
    return {
        "qT": (q * s).astype(np.float32),
        "kT": (n((D, T)) * (0.50 / np.sqrt(D)) / s).astype(np.float32),
        "vT": (n((DV, T)) / np.sqrt(DV) / v).astype(np.float32),
        "doT": (do * v).astype(np.float32),
        "lse": (np.log(N) + 0.12 + 0.1 * n((B, R, 1))).astype(np.float32),
        "delta": (0.3 * n((B, R, 1))).astype(np.float32),
        "rw": (np.random.uniform(0.5, 1.5, (B, R, 1)) * N / np.sqrt(R) * z).astype(np.float32),
        "qm": (q.transpose(0, 2, 1) / z).astype(np.float32),
        "offs": striped(idx),
    }


def reference(qT, kT, vT, doT, lse, delta, rw, qm, offs):
    idx = unstriped(offs)
    pick = lambda x: x[:, idx].reshape(x.shape[0], B, N).transpose(1, 0, 2)
    a = mxq(f64(qT), 1, "e4m3").transpose(0, 2, 1) @ mxq(pick(f64(kT)), 1, "e4m3")
    p = np.exp(a - f64(lse))
    dp = mxq(f64(doT), 1, "e5m2").transpose(0, 2, 1) @ mxq(pick(f64(vT)), 1, "e4m3")
    ds = f64(rw) * p * (dp - f64(delta))
    dk = mxq(f64(qm), 1, "e4m3").transpose(0, 2, 1) @ mxq(ds, 1, "e5m2")
    gk = np.zeros((D, T))
    gk[:, idx] = dk.transpose(1, 0, 2).reshape(D, B * N)
    out_0 = gk
    return (out_0,) + planes(out_0)

@@ -1,0 +1,197 @@
+from contextlib import ExitStack
+
+import concourse.mybir as mybir
+
+N, T, D, DV, R = 512, 2048, 512, 512, 1024
+FLOPS = 2 * R * N * (D + DV + D)
+
+F32 = mybir.dt.float32
+BF16 = mybir.dt.bfloat16
+I32 = mybir.dt.int32
+U32 = mybir.dt.uint32
+U16 = mybir.dt.uint16
+U8 = mybir.dt.uint8
+E4M3 = mybir.dt.float8_e4m3fn_x4
+E5M2 = mybir.dt.float8_e5m2_x4
+ACT = mybir.ActivationFunctionType
+ALU = mybir.AluOpType
+
+P = 128
+PACK = 4
+K_PASS = P * PACK
+PASSES = R // K_PASS
+CHUNKS = 4
+CW = T // CHUNKS
+
+
+def tile_attend_gat_pl_lse_k_kernel(tc, qT, kT, vT, doT, lse, delta, rw, qm, offs, out_0, out_1, out_2):
+    nc = tc.nc
+
+    def move(engine, out, in_):
+        if engine == "V":
+            nc.vector.tensor_copy(out=out, in_=in_)
+        else:
+            nc.scalar.copy(out=out, in_=in_)
+
+    with ExitStack() as ctx:
+        keep = ctx.enter_context(tc.tile_pool(name="keep", bufs=1))
+        psum = ctx.enter_context(tc.psum_pool(name="psum", bufs=1))
+        ring = ctx.enter_context(tc.psum_pool(name="ring", bufs=4))
+
+        offsets = keep.tile([P, N // 16], U16, name="offsets")
+        nc.sync.dma_start(offsets[:], offs)
+
+        q_raw = keep.tile([P, PACK, R], F32, name="q_raw", tag="q_then_p")
+        nc.sync.dma_start(out=q_raw[:], in_=qT[0].rearrange("(p j) r -> p j r", j=PACK))
+
+        rows = {}
+        for name, src in (("lse", lse), ("delta", delta), ("rw", rw)):
+            rows[name] = keep.tile([P, PASSES, PACK], F32, name=name + "_sb")
+            nc.scalar.dma_start(out=rows[name][:], in_=src[0].rearrange("(g p t) o -> p g (t o)", g=PASSES, t=PACK))
+
+        pools = {}
+        for name, src in (("k", kT), ("v", vT)):
+            for j in range(PACK):
+                pools[name, j] = keep.tile([P, T], F32, name="%s_plane%d" % (name, j), tag="%s%d" % (name, j), align_bytes=64)
+                nc.sync.dma_start(out=pools[name, j][:], in_=src.rearrange("(p j) c -> p j c", j=PACK)[:, j, :])
+
+        do_raw = []
+        for g in range(PASSES):
+            do_raw.append(keep.tile([P, PACK, K_PASS], F32, name="do_raw%d" % g, tag="do%d" % g, align_bytes=64))
+            nc.sync.dma_start(out=do_raw[g][:], in_=doT[0].rearrange("(p j) r -> p j r", j=PACK)[:, :, g * K_PASS:(g + 1) * K_PASS])
+        qm_raw = []
+        for g in range(PASSES):
+            qm_raw.append(keep.tile([P, PACK, D], F32, name="qm_raw%d" % g))
+            nc.sync.dma_start(out=qm_raw[g][:], in_=qm[0, g * K_PASS:(g + 1) * K_PASS, :].rearrange("(p t) d -> p t d", t=PACK))
+
+        windows = []
+        for j in range(PACK):
+            windows.append(keep.tile([P, T], F32, name="window%d" % j))
+            nc.vector.memset(windows[j][:], 0.0)
+
+        neg_lse = keep.tile([P, PASSES, PACK], F32, name="neg_lse")
+        nc.vector.tensor_scalar(out=neg_lse[:], in0=rows["lse"][:], scalar1=-1.0, scalar2=None, op0=ALU.mult)
+
+        def deal(engine, name, raw, h):
+            dealt = keep.tile([P, 2, P, PACK], BF16, name=name + "_dealt", align_bytes=64)
+            move(engine, dealt[:].rearrange("p u s j -> p s j u"),
+                 raw.rearrange("p j (s c) -> p s j c", c=PACK)[:, :, :, 2 * h:2 * h + 2])
+            return dealt
+
+        def quantize(name, grouped, width, fmt):
+            codes = keep.tile([P, width], U32, name=name + "_codes", align_bytes=64)
+            scales = keep.tile([P, width], U8, name=name + "_scales", align_bytes=64)
+            nc.vector.quantize_mx(out=codes[:].bitcast(fmt), scales=scales[:], in_=grouped)
+            return codes, scales, fmt
+
+        def quantize_dealt(name, dealt, fmt):
+            return quantize(name, dealt[:].rearrange("p u s j -> p (u s j)"), 2 * P, fmt)
+
+        def product(out, stationary, u, moving, start, stop):
+            cols = slice(u * P, (u + 1) * P)
+            nc.tensor.matmul_mx(out=out, lhsT=stationary[0][:, cols].bitcast(stationary[2]), lhsT_scale=stationary[1][:, cols],
+                                rhs=moving[0][:].bitcast(moving[2]), rhs_scale=moving[1][:], start=start, stop=stop)
+
+        def gather(name):
+            grouped = keep.tile([P, N, PACK], BF16, name=name + "_grouped", align_bytes=64)
+            for j in range(PACK):
+                nc.vector.tensor_copy(out=grouped[:, :, j], in_=pools[name, j][:].indirect(offsets[:]))
+            return quantize(name, grouped[:].rearrange("p n j -> p (n j)"), N, E4M3)
+
+        q_mx = {}
+        for g in range(PASSES):
+            for h in range(2):
+                name = "q%d%d" % (g, h)
+                q_mx[g, h] = quantize_dealt(name, deal("S", name, q_raw[:, :, g * K_PASS:(g + 1) * K_PASS], h), E4M3)
+        k_mx = gather("k")
+
+        gated = keep.tile([P, PASSES * PACK, N], F32, name="gated", tag="q_then_p")
+        for g in range(PASSES):
+            for t in range(PACK):
+                scores = ring.tile([P, N], F32, name="scores", tag="bank")
+                product(scores[:], q_mx[g, t // 2], t % 2, k_mx, True, True)
+                mine = gated[:, g * PACK + t, :]
+                nc.scalar.activation(out=mine, in_=scores[:], func=ACT.Exp, bias=neg_lse[:, g, t:t + 1], scale=1.0)
+                if g == 0:
+                    nc.vector.tensor_scalar(out=mine, in0=mine, scalar1=rows["rw"][:, g, t:t + 1], scalar2=None, op0=ALU.mult)
+                else:
+                    nc.scalar.activation(out=mine, in_=mine, func=ACT.Copy, scale=rows["rw"][:, g, t:t + 1])
+        v_mx = gather("v")
+
+        do_mx = {}
+        ds_flat = {}
+        ds_mx = {}
+        qm_mx = {}
+        qm_dealt = {}
+
+        def prepare_do(g, engines):
+            for h in range(2):
+                name = "do%d%d" % (g, h)
+                do_mx[g, h] = quantize_dealt(name, deal(engines[h], name, do_raw[g][:], h), E5M2)
+
+        def form_ds(g):
+            ds_flat[g] = keep.tile([P, PACK, N], BF16, name="ds_flat%d" % g)
+            for t in range(PACK):
+                dp = ring.tile([P, N], F32, name="dp", tag="bank")
+                product(dp[:], do_mx[g, t // 2], t % 2, v_mx, True, True)
+                nc.vector.scalar_tensor_tensor(out=ds_flat[g][:, t, :], in0=dp[:], scalar=rows["delta"][:, g, t:t + 1],
+                                               in1=gated[:, g * PACK + t, :], op0=ALU.subtract, op1=ALU.mult)
+
+        def quantize_ds(g, engines):
+            grouped = keep.tile([P, N, PACK], BF16, name="ds_grouped%d" % g, align_bytes=64)
+            for h in range(2):
+                cols = slice(h * N // 2, (h + 1) * N // 2)
+                move(engines[h], grouped[:, cols, :].rearrange("p (c i) t -> p c t i", i=4),
+                     ds_flat[g][:, :, cols].rearrange("p t (c i) -> p c t i", i=4))
+            ds_mx[g] = quantize("ds%d" % g, grouped[:].rearrange("p n t -> p (n t)"), N, E5M2)
+
+        def prepare_qm(g, h, engine):
+            name = "qm%d%d" % (g, h)
+            qm_mx[g, h] = quantize_dealt(name, deal(engine, name, qm_raw[g][:], h), E4M3)
+
+        prepare_do(0, "VS")
+        form_ds(0)
+        prepare_do(1, "SS")
+        form_ds(1)
+        quantize_ds(0, "SS")
+        quantize_ds(1, "SV")
+        prepare_qm(0, 0, "V")
+        prepare_qm(1, 0, "V")
+
+        out_rows = out_0.rearrange("(p j) c -> p j c", j=PACK)
+        dk_sb = keep.tile([P, T], F32, name="dk_sb", tag="k0", align_bytes=64)
+        pairs = []
+        for c in range(CHUNKS):
+            pairs.append(keep.tile([P, 2, CW, 2], BF16, name="pairs%d" % c, tag="v%d" % c, align_bytes=64))
+
+        def pair_up(j, engine):
+            for c in range(CHUNKS):
+                move(engine, pairs[c][:, j // 2, :, j % 2], windows[j][:, c * CW:(c + 1) * CW])
+
+        for j in range(PACK):
+            if j == 2:
+                prepare_qm(0, 1, "S")
+                prepare_qm(1, 1, "S")
+            dk = psum.tile([P, N], F32, name="dk%d" % j)
+            for g in range(PASSES):
+                product(dk[:], qm_mx[g, j // 2], j % 2, ds_mx[g], g == 0, g == PASSES - 1)
+            nc.scalar.copy(out=dk_sb[:, j * N:(j + 1) * N], in_=dk[:])
+            nc.vector.tensor_copy(out=windows[j][:].indirect(offsets[:]), in_=dk_sb[:, j * N:(j + 1) * N])
+            nc.sync.dma_start(out=out_rows[:, j, :], in_=windows[j][:])
+        for j in range(PACK):
+            pair_up(j, "S" if j < 2 else "V")
+
+        out_codes = keep.tile([P, T], U32, name="out_codes", tag="k3", align_bytes=64)
+        out_scales = keep.tile([P, T], U8, name="out_scales", align_bytes=64)
+        words = out_1[0].rearrange("p c l -> p (c l)").bitcast(I32)
+        for c in range(CHUNKS):
+            cols = slice(c * CW, (c + 1) * CW)
+            grouped = keep.tile([P, CW, 2, 2], BF16, name="grouped_out%d" % c, tag=("k1", "k2", "do0", "do1")[c], align_bytes=64)
+            move("VVSS"[c], grouped[:].rearrange("p (c i) u e -> p c u i e", i=4),
+                 pairs[c][:].rearrange("p u (c i) e -> p c u i e", i=4))
+            nc.vector.quantize_mx(out=out_codes[:, cols].bitcast(E4M3), scales=out_scales[:, cols],
+                                  in_=grouped[:].rearrange("p n u e -> p (n u e)"))
+            nc.sync.dma_start(out=words[:, cols], in_=out_codes[:, cols].bitcast(I32))
+        scale_rows = out_2[0].bitcast(I32)
+        for quad in range(4):
+            nc.scalar.dma_start(out=scale_rows[4 * quad:4 * quad + 4, :], in_=out_scales[32 * quad:32 * quad + 4, :].bitcast(I32))

@@ -41,6 +41,14 @@ def tile_attend_gat_pl_lse_k_kernel(tc, qT, kT, vT, doT, lse, delta, rw, qm, off
         offsets = keep.tile([P, N // 16], U16, name="offsets")
         nc.sync.dma_start(offsets[:], offs)
 
+        pools = {}
+
+        def load_pool(name, src):
+            for j in range(PACK):
+                pools[name, j] = keep.tile([P, T], F32, name="%s_plane%d" % (name, j), tag="%s%d" % (name, j), align_bytes=64)
+                nc.sync.dma_start(out=pools[name, j][:], in_=src.rearrange("(p j) c -> p j c", j=PACK)[:, j, :])
+
+        load_pool("k", kT)
         q_raw = keep.tile([P, PACK, R], F32, name="q_raw", tag="q_then_p")
         nc.sync.dma_start(out=q_raw[:], in_=qT[0].rearrange("(p j) r -> p j r", j=PACK))
 
@@ -49,12 +57,7 @@ def tile_attend_gat_pl_lse_k_kernel(tc, qT, kT, vT, doT, lse, delta, rw, qm, off
             rows[name] = keep.tile([P, PASSES, PACK], F32, name=name + "_sb")
             nc.scalar.dma_start(out=rows[name][:], in_=src[0].rearrange("(g p t) o -> p g (t o)", g=PASSES, t=PACK))
 
-        pools = {}
-        for name, src in (("k", kT), ("v", vT)):
-            for j in range(PACK):
-                pools[name, j] = keep.tile([P, T], F32, name="%s_plane%d" % (name, j), tag="%s%d" % (name, j), align_bytes=64)
-                nc.sync.dma_start(out=pools[name, j][:], in_=src.rearrange("(p j) c -> p j c", j=PACK)[:, j, :])
-
+        load_pool("v", vT)
         do_raw = []
         for g in range(PASSES):
             do_raw.append(keep.tile([P, PACK, K_PASS], F32, name="do_raw%d" % g, tag="do%d" % g, align_bytes=64))
@@ -93,17 +96,20 @@ def tile_attend_gat_pl_lse_k_kernel(tc, qT, kT, vT, doT, lse, delta, rw, qm, off
                                 rhs=moving[0][:].bitcast(moving[2]), rhs_scale=moving[1][:], start=start, stop=stop)
 
         def gather(name):
-            grouped = keep.tile([P, N, PACK], BF16, name=name + "_grouped", align_bytes=64)
+            picked = keep.tile([P, PACK, N], F32, name=name + "_picked", tag="picked")
             for j in range(PACK):
-                nc.vector.tensor_copy(out=grouped[:, :, j], in_=pools[name, j][:].indirect(offsets[:]))
+                nc.vector.tensor_copy(out=picked[:, j, :], in_=pools[name, j][:].indirect(offsets[:]))
+            grouped = keep.tile([P, N, PACK], BF16, name=name + "_grouped", align_bytes=64)
+            nc.vector.tensor_copy(out=grouped[:].rearrange("p (c i) j -> p c j i", i=4),
+                                  in_=picked[:].rearrange("p j (c i) -> p c j i", i=4))
             return quantize(name, grouped[:].rearrange("p n j -> p (n j)"), N, E4M3)
 
+        k_mx = gather("k")
         q_mx = {}
         for g in range(PASSES):
             for h in range(2):
                 name = "q%d%d" % (g, h)
-                q_mx[g, h] = quantize_dealt(name, deal("S", name, q_raw[:, :, g * K_PASS:(g + 1) * K_PASS], h), E4M3)
-        k_mx = gather("k")
+                q_mx[g, h] = quantize_dealt(name, deal("VVVS"[2 * g + h], name, q_raw[:, :, g * K_PASS:(g + 1) * K_PASS], h), E4M3)
 
         gated = keep.tile([P, PASSES * PACK, N], F32, name="gated", tag="q_then_p")
         for g in range(PASSES):
@@ -149,14 +155,14 @@ def tile_attend_gat_pl_lse_k_kernel(tc, qT, kT, vT, doT, lse, delta, rw, qm, off
             name = "qm%d%d" % (g, h)
             qm_mx[g, h] = quantize_dealt(name, deal(engine, name, qm_raw[g][:], h), E4M3)
 
-        prepare_do(0, "VS")
+        prepare_do(0, "SS")
         form_ds(0)
         prepare_do(1, "SS")
         form_ds(1)
+        prepare_qm(0, 0, "S")
         quantize_ds(0, "SS")
-        quantize_ds(1, "SV")
-        prepare_qm(0, 0, "V")
-        prepare_qm(1, 0, "V")
+        quantize_ds(1, "VV")
+        prepare_qm(1, 0, "S")
 
         out_rows = out_0.rearrange("(p j) c -> p j c", j=PACK)
         dk_sb = keep.tile([P, T], F32, name="dk_sb", tag="k0", align_bytes=64)
@@ -164,9 +170,9 @@ def tile_attend_gat_pl_lse_k_kernel(tc, qT, kT, vT, doT, lse, delta, rw, qm, off
         for c in range(CHUNKS):
             pairs.append(keep.tile([P, 2, CW, 2], BF16, name="pairs%d" % c, tag="v%d" % c, align_bytes=64))
 
-        def pair_up(j, engine):
+        def pair_up(j, engines):
             for c in range(CHUNKS):
-                move(engine, pairs[c][:, j // 2, :, j % 2], windows[j][:, c * CW:(c + 1) * CW])
+                move(engines[c], pairs[c][:, j // 2, :, j % 2], windows[j][:, c * CW:(c + 1) * CW])
 
         for j in range(PACK):
             if j == 2:
@@ -175,11 +181,11 @@ def tile_attend_gat_pl_lse_k_kernel(tc, qT, kT, vT, doT, lse, delta, rw, qm, off
             dk = psum.tile([P, N], F32, name="dk%d" % j)
             for g in range(PASSES):
                 product(dk[:], qm_mx[g, j // 2], j % 2, ds_mx[g], g == 0, g == PASSES - 1)
-            nc.scalar.copy(out=dk_sb[:, j * N:(j + 1) * N], in_=dk[:])
+            move("VSSS"[j], dk_sb[:, j * N:(j + 1) * N], dk[:])
             nc.vector.tensor_copy(out=windows[j][:].indirect(offsets[:]), in_=dk_sb[:, j * N:(j + 1) * N])
             nc.sync.dma_start(out=out_rows[:, j, :], in_=windows[j][:])
         for j in range(PACK):
-            pair_up(j, "S" if j < 2 else "V")
+            pair_up(j, ("SSSS", "SSSS", "VVVV", "VVVV")[j])
 
         out_codes = keep.tile([P, T], U32, name="out_codes", tag="k3", align_bytes=64)
         out_scales = keep.tile([P, T], U8, name="out_scales", align_bytes=64)

@@ -95,16 +95,18 @@ def tile_attend_gat_pl_lse_k_kernel(tc, qT, kT, vT, doT, lse, delta, rw, qm, off
             nc.tensor.matmul_mx(out=out, lhsT=stationary[0][:, cols].bitcast(stationary[2]), lhsT_scale=stationary[1][:, cols],
                                 rhs=moving[0][:].bitcast(moving[2]), rhs_scale=moving[1][:], start=start, stop=stop)
 
-        def gather(name):
+        def gather(name, engines):
             picked = keep.tile([P, PACK, N], F32, name=name + "_picked", tag="picked")
             for j in range(PACK):
                 nc.vector.tensor_copy(out=picked[:, j, :], in_=pools[name, j][:].indirect(offsets[:]))
             grouped = keep.tile([P, N, PACK], BF16, name=name + "_grouped", align_bytes=64)
-            nc.vector.tensor_copy(out=grouped[:].rearrange("p (c i) j -> p c j i", i=4),
-                                  in_=picked[:].rearrange("p j (c i) -> p c j i", i=4))
+            for h in range(2):
+                cols = slice(h * N // 2, (h + 1) * N // 2)
+                move(engines[h], grouped[:, cols, :].rearrange("p (c i) j -> p c j i", i=4),
+                     picked[:, :, cols].rearrange("p j (c i) -> p c j i", i=4))
             return quantize(name, grouped[:].rearrange("p n j -> p (n j)"), N, E4M3)
 
-        k_mx = gather("k")
+        k_mx = gather("k", "VV")
         q_mx = {}
         for g in range(PASSES):
             for h in range(2):
@@ -122,7 +124,7 @@ def tile_attend_gat_pl_lse_k_kernel(tc, qT, kT, vT, doT, lse, delta, rw, qm, off
                     nc.vector.tensor_scalar(out=mine, in0=mine, scalar1=rows["rw"][:, g, t:t + 1], scalar2=None, op0=ALU.mult)
                 else:
                     nc.scalar.activation(out=mine, in_=mine, func=ACT.Copy, scale=rows["rw"][:, g, t:t + 1])
-        v_mx = gather("v")
+        v_mx = gather("v", "SV")
 
         do_mx = {}
         ds_flat = {}
@@ -155,7 +157,7 @@ def tile_attend_gat_pl_lse_k_kernel(tc, qT, kT, vT, doT, lse, delta, rw, qm, off
             name = "qm%d%d" % (g, h)
             qm_mx[g, h] = quantize_dealt(name, deal(engine, name, qm_raw[g][:], h), E4M3)
 
-        prepare_do(0, "SS")
+        prepare_do(0, "VS")
         form_ds(0)
         prepare_do(1, "SS")
         form_ds(1)
@@ -166,38 +168,51 @@ def tile_attend_gat_pl_lse_k_kernel(tc, qT, kT, vT, doT, lse, delta, rw, qm, off
 
         out_rows = out_0.rearrange("(p j) c -> p j c", j=PACK)
         dk_sb = keep.tile([P, T], F32, name="dk_sb", tag="k0", align_bytes=64)
-        pairs = []
-        for c in range(CHUNKS):
-            pairs.append(keep.tile([P, 2, CW, 2], BF16, name="pairs%d" % c, tag="v%d" % c, align_bytes=64))
+        flat = []
+        for half in range(2):
+            flat.append(keep.tile([P, PACK, T // 2], BF16, name="flat%d" % half, tag="v%d" % half, align_bytes=64))
 
-        def pair_up(j, engines):
-            for c in range(CHUNKS):
-                move(engines[c], pairs[c][:, j // 2, :, j % 2], windows[j][:, c * CW:(c + 1) * CW])
+        def round_plane(engine, j, first, width):
+            half, at = divmod(first, T // 2)
+            move(engine, flat[half][:, j, at:at + width], windows[j][:, first:first + width])
 
         for j in range(PACK):
             if j == 2:
                 prepare_qm(0, 1, "S")
-                prepare_qm(1, 1, "S")
+                prepare_qm(1, 1, "V")
             dk = psum.tile([P, N], F32, name="dk%d" % j)
             for g in range(PASSES):
                 product(dk[:], qm_mx[g, j // 2], j % 2, ds_mx[g], g == 0, g == PASSES - 1)
-            move("VSSS"[j], dk_sb[:, j * N:(j + 1) * N], dk[:])
+            move("SSSS"[j], dk_sb[:, j * N:(j + 1) * N], dk[:])
             nc.vector.tensor_copy(out=windows[j][:].indirect(offsets[:]), in_=dk_sb[:, j * N:(j + 1) * N])
             nc.sync.dma_start(out=out_rows[:, j, :], in_=windows[j][:])
-        for j in range(PACK):
-            pair_up(j, ("SSSS", "SSSS", "VVVV", "VVVV")[j])
+        for j in (0, 1):
+            for c in (2, 3, 0, 1):
+                round_plane("S", j, c * CW, CW)
+        for first, width in ((2 * CW, CW), (3 * CW, CW), (0, 2 * CW)):
+            for j in (2, 3):
+                round_plane("V", j, first, width)
 
         out_codes = keep.tile([P, T], U32, name="out_codes", tag="k3", align_bytes=64)
         out_scales = keep.tile([P, T], U8, name="out_scales", align_bytes=64)
         words = out_1[0].rearrange("p c l -> p (c l)").bitcast(I32)
+        scale_rows = out_2[0].bitcast(I32)
+
+        def store_scales(first, width, queues):
+            for quad in range(4):
+                queues[quad].dma_start(out=scale_rows[4 * quad:4 * quad + 4, first // 4:(first + width) // 4],
+                                       in_=out_scales[32 * quad:32 * quad + 4, first:first + width].bitcast(I32))
+
+        grouped_out = {}
+        for c in (2, 3, 0, 1):
+            grouped_out[c] = keep.tile([P, CW, PACK], BF16, name="grouped_out%d" % c, tag=("k1", "k2", "do0", "do1")[c], align_bytes=64)
+            move("VVSS"[c], grouped_out[c][:].rearrange("p (c i) j -> p c j i", i=4),
+                 flat[c // 2][:, :, (c % 2) * CW:(c % 2 + 1) * CW].rearrange("p j (c i) -> p c j i", i=4))
         for c in range(CHUNKS):
             cols = slice(c * CW, (c + 1) * CW)
-            grouped = keep.tile([P, CW, 2, 2], BF16, name="grouped_out%d" % c, tag=("k1", "k2", "do0", "do1")[c], align_bytes=64)
-            move("VVSS"[c], grouped[:].rearrange("p (c i) u e -> p c u i e", i=4),
-                 pairs[c][:].rearrange("p u (c i) e -> p c u i e", i=4))
             nc.vector.quantize_mx(out=out_codes[:, cols].bitcast(E4M3), scales=out_scales[:, cols],
-                                  in_=grouped[:].rearrange("p n u e -> p (n u e)"))
+                                  in_=grouped_out[c][:].rearrange("p n j -> p (n j)"))
             nc.sync.dma_start(out=words[:, cols], in_=out_codes[:, cols].bitcast(I32))
-        scale_rows = out_2[0].bitcast(I32)
-        for quad in range(4):
-            nc.scalar.dma_start(out=scale_rows[4 * quad:4 * quad + 4, :], in_=out_scales[32 * quad:32 * quad + 4, :].bitcast(I32))
+            if c == CHUNKS - 2:
+                store_scales(0, 3 * CW, (nc.sync, nc.sync, nc.sync, nc.sync))
+        store_scales(3 * CW, CW, (nc.sync, nc.sync, nc.scalar, nc.scalar))

@@ -84,7 +84,9 @@ def tile_attend_gat_pl_lse_k_kernel(tc, qT, kT, vT, doT, lse, delta, rw, qm, off
         def quantize(name, grouped, width, fmt):
             codes = keep.tile([P, width], U32, name=name + "_codes", align_bytes=64)
             scales = keep.tile([P, width], U8, name=name + "_scales", align_bytes=64)
-            nc.vector.quantize_mx(out=codes[:].bitcast(fmt), scales=scales[:], in_=grouped)
+            for first in range(0, width, 2 * P):
+                nc.vector.quantize_mx(out=codes[:, first:first + 2 * P].bitcast(fmt), scales=scales[:, first:first + 2 * P],
+                                      in_=grouped[:, PACK * first:PACK * (first + 2 * P)])
             return codes, scales, fmt
 
         def quantize_dealt(name, dealt, fmt):
@@ -124,7 +126,7 @@ def tile_attend_gat_pl_lse_k_kernel(tc, qT, kT, vT, doT, lse, delta, rw, qm, off
                     nc.vector.tensor_scalar(out=mine, in0=mine, scalar1=rows["rw"][:, g, t:t + 1], scalar2=None, op0=ALU.mult)
                 else:
                     nc.scalar.activation(out=mine, in_=mine, func=ACT.Copy, scale=rows["rw"][:, g, t:t + 1])
-        v_mx = gather("v", "SV")
+        v_mx = gather("v", "VV")
 
         do_mx = {}
         ds_flat = {}
@@ -157,7 +159,7 @@ def tile_attend_gat_pl_lse_k_kernel(tc, qT, kT, vT, doT, lse, delta, rw, qm, off
             name = "qm%d%d" % (g, h)
             qm_mx[g, h] = quantize_dealt(name, deal(engine, name, qm_raw[g][:], h), E4M3)
 
-        prepare_do(0, "VS")
+        prepare_do(0, "SS")
         form_ds(0)
         prepare_do(1, "SS")
         form_ds(1)
@@ -179,11 +181,11 @@ def tile_attend_gat_pl_lse_k_kernel(tc, qT, kT, vT, doT, lse, delta, rw, qm, off
         for j in range(PACK):
             if j == 2:
                 prepare_qm(0, 1, "S")
-                prepare_qm(1, 1, "V")
+                prepare_qm(1, 1, "S")
             dk = psum.tile([P, N], F32, name="dk%d" % j)
             for g in range(PASSES):
                 product(dk[:], qm_mx[g, j // 2], j % 2, ds_mx[g], g == 0, g == PASSES - 1)
-            move("SSSS"[j], dk_sb[:, j * N:(j + 1) * N], dk[:])
+            move("VSSS"[j], dk_sb[:, j * N:(j + 1) * N], dk[:])
             nc.vector.tensor_copy(out=windows[j][:].indirect(offsets[:]), in_=dk_sb[:, j * N:(j + 1) * N])
             nc.sync.dma_start(out=out_rows[:, j, :], in_=windows[j][:])
         for j in (0, 1):
@@ -213,6 +215,4 @@ def tile_attend_gat_pl_lse_k_kernel(tc, qT, kT, vT, doT, lse, delta, rw, qm, off
             nc.vector.quantize_mx(out=out_codes[:, cols].bitcast(E4M3), scales=out_scales[:, cols],
                                   in_=grouped_out[c][:].rearrange("p n j -> p (n j)"))
             nc.sync.dma_start(out=words[:, cols], in_=out_codes[:, cols].bitcast(I32))
-            if c == CHUNKS - 2:
-                store_scales(0, 3 * CW, (nc.sync, nc.sync, nc.sync, nc.sync))
-        store_scales(3 * CW, CW, (nc.sync, nc.sync, nc.scalar, nc.scalar))
+        store_scales(0, T, (nc.scalar, nc.scalar, nc.scalar, nc.scalar))

@@ -58,10 +58,12 @@ def tile_attend_gat_pl_lse_k_kernel(tc, qT, kT, vT, doT, lse, delta, rw, qm, off
             nc.scalar.dma_start(out=rows[name][:], in_=src[0].rearrange("(g p t) o -> p g (t o)", g=PASSES, t=PACK))
 
         load_pool("v", vT)
-        do_raw = []
+        do_raw = {}
         for g in range(PASSES):
-            do_raw.append(keep.tile([P, PACK, K_PASS], F32, name="do_raw%d" % g, tag="do%d" % g, align_bytes=64))
-            nc.sync.dma_start(out=do_raw[g][:], in_=doT[0].rearrange("(p j) r -> p j r", j=PACK)[:, :, g * K_PASS:(g + 1) * K_PASS])
+            for a in range(2):
+                first = g * K_PASS + a * K_PASS // 2
+                do_raw[g, a] = keep.tile([P, PACK, K_PASS // 2], F32, name="do_raw%d%d" % (g, a), align_bytes=64)
+                nc.sync.dma_start(out=do_raw[g, a][:], in_=doT[0].rearrange("(p j) r -> p j r", j=PACK)[:, :, first:first + K_PASS // 2])
         qm_raw = []
         for g in range(PASSES):
             qm_raw.append(keep.tile([P, PACK, D], F32, name="qm_raw%d" % g))
@@ -132,41 +134,63 @@ def tile_attend_gat_pl_lse_k_kernel(tc, qT, kT, vT, doT, lse, delta, rw, qm, off
         ds_flat = {}
         ds_mx = {}
         qm_mx = {}
-        qm_dealt = {}
 
-        def prepare_do(g, engines):
+        def prepare_do(g):
+            dealt = []
             for h in range(2):
-                name = "do%d%d" % (g, h)
-                do_mx[g, h] = quantize_dealt(name, deal(engines[h], name, do_raw[g][:], h), E5M2)
+                dealt.append(keep.tile([P, 2, P, PACK], BF16, name="do%d%d_dealt" % (g, h), tag="do%d%d" % (g, h), align_bytes=64))
+            for a in range(2):
+                for h in range(2):
+                    move("S", dealt[h][:, :, a * P // 2:(a + 1) * P // 2, :].rearrange("p u s j -> p s j u"),
+                         do_raw[g, a][:].rearrange("p j (s c) -> p s j c", c=PACK)[:, :, :, 2 * h:2 * h + 2])
+            for h in range(2):
+                do_mx[g, h] = quantize_dealt("do%d%d" % (g, h), dealt[h], E5M2)
 
-        def form_ds(g):
-            ds_flat[g] = keep.tile([P, PACK, N], BF16, name="ds_flat%d" % g)
+        def form_ds(g, parts):
+            dp = []
             for t in range(PACK):
-                dp = ring.tile([P, N], F32, name="dp", tag="bank")
-                product(dp[:], do_mx[g, t // 2], t % 2, v_mx, True, True)
-                nc.vector.scalar_tensor_tensor(out=ds_flat[g][:, t, :], in0=dp[:], scalar=rows["delta"][:, g, t:t + 1],
-                                               in1=gated[:, g * PACK + t, :], op0=ALU.subtract, op1=ALU.mult)
+                dp.append(ring.tile([P, N], F32, name="dp", tag="bank"))
+                product(dp[t][:], do_mx[g, t // 2], t % 2, v_mx, True, True)
+            width = N // parts
+            for h in range(parts):
+                cols = slice(h * width, (h + 1) * width)
+                ds_flat[g, h] = keep.tile([P, PACK, width], BF16, name="ds_flat%d%d" % (g, h))
+                for t in range(PACK):
+                    nc.vector.scalar_tensor_tensor(out=ds_flat[g, h][:, t, :], in0=dp[t][:, cols], scalar=rows["delta"][:, g, t:t + 1],
+                                                   in1=gated[:, g * PACK + t, cols], op0=ALU.subtract, op1=ALU.mult)
 
-        def quantize_ds(g, engines):
-            grouped = keep.tile([P, N, PACK], BF16, name="ds_grouped%d" % g, align_bytes=64)
+        def regroup_ds(g, h, engine, flat_half):
+            grouped = keep.tile([P, N // 2, PACK], BF16, name="ds_grouped%d%d" % (g, h), tag="do%d%d" % (1 - g, 1 - h), align_bytes=64)
+            if engine == "G":
+                nc.gpsimd.tensor_scalar(out=grouped[:], in0=flat_half.rearrange("p t n -> p n t"),
+                                        scalar1=1.0, scalar2=0.0, op0=ALU.mult, op1=ALU.add)
+            else:
+                move(engine, grouped[:].rearrange("p (c i) t -> p c t i", i=4), flat_half.rearrange("p t (c i) -> p c t i", i=4))
+            return grouped
+
+        def quantize_ds(g, halves):
+            codes = keep.tile([P, N], U32, name="ds%d_codes" % g, align_bytes=64)
+            scales = keep.tile([P, N], U8, name="ds%d_scales" % g, align_bytes=64)
             for h in range(2):
                 cols = slice(h * N // 2, (h + 1) * N // 2)
-                move(engines[h], grouped[:, cols, :].rearrange("p (c i) t -> p c t i", i=4),
-                     ds_flat[g][:, :, cols].rearrange("p t (c i) -> p c t i", i=4))
-            ds_mx[g] = quantize("ds%d" % g, grouped[:].rearrange("p n t -> p (n t)"), N, E5M2)
+                nc.vector.quantize_mx(out=codes[:, cols].bitcast(E5M2), scales=scales[:, cols], in_=halves[h][:].rearrange("p n t -> p (n t)"))
+            ds_mx[g] = codes, scales, E5M2
 
         def prepare_qm(g, h, engine):
             name = "qm%d%d" % (g, h)
             qm_mx[g, h] = quantize_dealt(name, deal(engine, name, qm_raw[g][:], h), E4M3)
 
-        prepare_do(0, "SS")
-        form_ds(0)
-        prepare_do(1, "SS")
-        form_ds(1)
+        prepare_do(0)
+        prepare_do(1)
+        form_ds(0, 1)
+        form_ds(1, 2)
+        quantize_ds(0, [regroup_ds(0, h, "G", ds_flat[0, 0][:, :, h * N // 2:(h + 1) * N // 2]) for h in range(2)])
         prepare_qm(0, 0, "S")
-        quantize_ds(0, "SS")
-        quantize_ds(1, "VV")
+        last_halves = [regroup_ds(1, h, "SV"[h], ds_flat[1, h][:]) for h in range(2)]
         prepare_qm(1, 0, "S")
+        quantize_ds(1, last_halves)
+        prepare_qm(0, 1, "S")
+        prepare_qm(1, 1, "S")
 
         out_rows = out_0.rearrange("(p j) c -> p j c", j=PACK)
         dk_sb = keep.tile([P, T], F32, name="dk_sb", tag="k0", align_bytes=64)
@@ -179,21 +203,19 @@ def tile_attend_gat_pl_lse_k_kernel(tc, qT, kT, vT, doT, lse, delta, rw, qm, off
             move(engine, flat[half][:, j, at:at + width], windows[j][:, first:first + width])
 
         for j in range(PACK):
-            if j == 2:
-                prepare_qm(0, 1, "S")
-                prepare_qm(1, 1, "S")
             dk = psum.tile([P, N], F32, name="dk%d" % j)
             for g in range(PASSES):
                 product(dk[:], qm_mx[g, j // 2], j % 2, ds_mx[g], g == 0, g == PASSES - 1)
-            move("VSSS"[j], dk_sb[:, j * N:(j + 1) * N], dk[:])
+            move("SSSS"[j], dk_sb[:, j * N:(j + 1) * N], dk[:])
             nc.vector.tensor_copy(out=windows[j][:].indirect(offsets[:]), in_=dk_sb[:, j * N:(j + 1) * N])
             nc.sync.dma_start(out=out_rows[:, j, :], in_=windows[j][:])
         for j in (0, 1):
-            for c in (2, 3, 0, 1):
-                round_plane("S", j, c * CW, CW)
-        for first, width in ((2 * CW, CW), (3 * CW, CW), (0, 2 * CW)):
-            for j in (2, 3):
-                round_plane("V", j, first, width)
+            for half in (1, 0):
+                round_plane("S", j, half * 2 * CW, 2 * CW)
+        round_plane("V", 3, 2 * CW, 2 * CW)
+        round_plane("S", 2, 2 * CW, 2 * CW)
+        for j in (2, 3):
+            round_plane("V", j, 0, 2 * CW)
 
         out_codes = keep.tile([P, T], U32, name="out_codes", tag="k3", align_bytes=64)
         out_scales = keep.tile([P, T], U8, name="out_scales", align_bytes=64)
@@ -207,7 +229,7 @@ def tile_attend_gat_pl_lse_k_kernel(tc, qT, kT, vT, doT, lse, delta, rw, qm, off
 
         grouped_out = {}
         for c in (2, 3, 0, 1):
-            grouped_out[c] = keep.tile([P, CW, PACK], BF16, name="grouped_out%d" % c, tag=("k1", "k2", "do0", "do1")[c], align_bytes=64)
+            grouped_out[c] = keep.tile([P, CW, PACK], BF16, name="grouped_out%d" % c, tag=("k1", "k2", "v2", "v3")[c], align_bytes=64)
             move("VVSS"[c], grouped_out[c][:].rearrange("p (c i) j -> p c j i", i=4),
                  flat[c // 2][:, :, (c % 2) * CW:(c % 2 + 1) * CW].rearrange("p j (c i) -> p c j i", i=4))
         for c in range(CHUNKS):

@@ -1,6 +1,7 @@
 from contextlib import ExitStack
 
 import concourse.mybir as mybir
+from concourse.masks import make_identity
 
 N, T, D, DV, R = 512, 2048, 512, 512, 1024
 FLOPS = 2 * R * N * (D + DV + D)
@@ -39,7 +40,6 @@ def tile_attend_gat_pl_lse_k_kernel(tc, qT, kT, vT, doT, lse, delta, rw, qm, off
         ring = ctx.enter_context(tc.psum_pool(name="ring", bufs=4))
 
         offsets = keep.tile([P, N // 16], U16, name="offsets")
-        nc.sync.dma_start(offsets[:], offs)
 
         pools = {}
 
@@ -47,15 +47,26 @@ def tile_attend_gat_pl_lse_k_kernel(tc, qT, kT, vT, doT, lse, delta, rw, qm, off
             for j in range(PACK):
                 pools[name, j] = keep.tile([P, T], F32, name="%s_plane%d" % (name, j), tag="%s%d" % (name, j), align_bytes=64)
                 nc.sync.dma_start(out=pools[name, j][:], in_=src.rearrange("(p j) c -> p j c", j=PACK)[:, j, :])
+                if (name, j) == ("k", 0):
+                    nc.sync.dma_start(offsets[:], offs)
 
         load_pool("k", kT)
         q_raw = keep.tile([P, PACK, R], F32, name="q_raw", tag="q_then_p")
         nc.sync.dma_start(out=q_raw[:], in_=qT[0].rearrange("(p j) r -> p j r", j=PACK))
 
-        rows = {}
-        for name, src in (("lse", lse), ("delta", delta), ("rw", rw)):
-            rows[name] = keep.tile([P, PASSES, PACK], F32, name=name + "_sb")
-            nc.scalar.dma_start(out=rows[name][:], in_=src[0].rearrange("(g p t) o -> p g (t o)", g=PASSES, t=PACK))
+        vectors = keep.tile([P, K_PASS], F32, name="vectors")
+        nc.vector.memset(vectors[:], 0.0)
+        for i, src in enumerate((lse, delta, rw)):
+            nc.scalar.dma_start(out=vectors[PASSES * i:PASSES * (i + 1), :], in_=src[0].rearrange("(g r) o -> g (r o)", g=PASSES))
+        identity = keep.tile([P, P], F32, name="identity")
+        make_identity(nc, identity[:])
+        turned = ring.tile([P, PACK, P], F32, name="turned", tag="bank")
+        for t in range(PACK):
+            nc.tensor.transpose(turned[:, t, :], vectors[:, t::PACK], identity[:])
+        neg_lse = keep.tile([P, PACK, PASSES], F32, name="neg_lse")
+        nc.vector.tensor_scalar(out=neg_lse[:], in0=turned[:, :, 0:PASSES], scalar1=-1.0, scalar2=None, op0=ALU.mult)
+        delta_rw = keep.tile([P, PACK, 2 * PASSES], F32, name="delta_rw")
+        nc.vector.tensor_copy(out=delta_rw[:], in_=turned[:, :, PASSES:3 * PASSES])
 
         load_pool("v", vT)
         do_raw = {}
@@ -73,9 +84,6 @@ def tile_attend_gat_pl_lse_k_kernel(tc, qT, kT, vT, doT, lse, delta, rw, qm, off
         for j in range(PACK):
             windows.append(keep.tile([P, T], F32, name="window%d" % j))
             nc.vector.memset(windows[j][:], 0.0)
-
-        neg_lse = keep.tile([P, PASSES, PACK], F32, name="neg_lse")
-        nc.vector.tensor_scalar(out=neg_lse[:], in0=rows["lse"][:], scalar1=-1.0, scalar2=None, op0=ALU.mult)
 
         def deal(engine, name, raw, h):
             dealt = keep.tile([P, 2, P, PACK], BF16, name=name + "_dealt", align_bytes=64)
@@ -123,11 +131,11 @@ def tile_attend_gat_pl_lse_k_kernel(tc, qT, kT, vT, doT, lse, delta, rw, qm, off
                 scores = ring.tile([P, N], F32, name="scores", tag="bank")
                 product(scores[:], q_mx[g, t // 2], t % 2, k_mx, True, True)
                 mine = gated[:, g * PACK + t, :]
-                nc.scalar.activation(out=mine, in_=scores[:], func=ACT.Exp, bias=neg_lse[:, g, t:t + 1], scale=1.0)
+                nc.scalar.activation(out=mine, in_=scores[:], func=ACT.Exp, bias=neg_lse[:, t, g:g + 1], scale=1.0)
                 if g == 0:
-                    nc.vector.tensor_scalar(out=mine, in0=mine, scalar1=rows["rw"][:, g, t:t + 1], scalar2=None, op0=ALU.mult)
+                    nc.vector.tensor_scalar(out=mine, in0=mine, scalar1=delta_rw[:, t, PASSES + g:PASSES + g + 1], scalar2=None, op0=ALU.mult)
                 else:
-                    nc.scalar.activation(out=mine, in_=mine, func=ACT.Copy, scale=rows["rw"][:, g, t:t + 1])
+                    nc.scalar.activation(out=mine, in_=mine, func=ACT.Copy, scale=delta_rw[:, t, PASSES + g:PASSES + g + 1])
         v_mx = gather("v", "VV")
 
         do_mx = {}
@@ -156,7 +164,7 @@ def tile_attend_gat_pl_lse_k_kernel(tc, qT, kT, vT, doT, lse, delta, rw, qm, off
                 cols = slice(h * width, (h + 1) * width)
                 ds_flat[g, h] = keep.tile([P, PACK, width], BF16, name="ds_flat%d%d" % (g, h))
                 for t in range(PACK):
-                    nc.vector.scalar_tensor_tensor(out=ds_flat[g, h][:, t, :], in0=dp[t][:, cols], scalar=rows["delta"][:, g, t:t + 1],
+                    nc.vector.scalar_tensor_tensor(out=ds_flat[g, h][:, t, :], in0=dp[t][:, cols], scalar=delta_rw[:, t, g:g + 1],
                                                    in1=gated[:, g * PACK + t, cols], op0=ALU.subtract, op1=ALU.mult)
 
         def regroup_ds(g, h, engine, flat_half):
@@ -236,5 +244,7 @@ def tile_attend_gat_pl_lse_k_kernel(tc, qT, kT, vT, doT, lse, delta, rw, qm, off
             cols = slice(c * CW, (c + 1) * CW)
             nc.vector.quantize_mx(out=out_codes[:, cols].bitcast(E4M3), scales=out_scales[:, cols],
                                   in_=grouped_out[c][:].rearrange("p n j -> p (n j)"))
-            nc.sync.dma_start(out=words[:, cols], in_=out_codes[:, cols].bitcast(I32))
+            if c >= 1:
+                stored = slice(0, 2 * CW) if c == 1 else cols
+                nc.sync.dma_start(out=words[:, stored], in_=out_codes[:, stored].bitcast(I32))
         store_scales(0, T, (nc.scalar, nc.scalar, nc.scalar, nc.scalar))

@@ -31,6 +31,8 @@ def tile_attend_gat_pl_lse_k_kernel(tc, qT, kT, vT, doT, lse, delta, rw, qm, off
     def move(engine, out, in_):
         if engine == "V":
             nc.vector.tensor_copy(out=out, in_=in_)
+        elif engine == "G":
+            nc.gpsimd.tensor_scalar(out=out, in0=in_, scalar1=1.0, scalar2=-0.0, op0=ALU.mult, op1=ALU.add)
         else:
             nc.scalar.copy(out=out, in_=in_)
 
@@ -43,21 +45,22 @@ def tile_attend_gat_pl_lse_k_kernel(tc, qT, kT, vT, doT, lse, delta, rw, qm, off
 
         pools = {}
 
-        def load_pool(name, src):
-            for j in range(PACK):
-                pools[name, j] = keep.tile([P, T], F32, name="%s_plane%d" % (name, j), tag="%s%d" % (name, j), align_bytes=64)
-                nc.sync.dma_start(out=pools[name, j][:], in_=src.rearrange("(p j) c -> p j c", j=PACK)[:, j, :])
-                if (name, j) == ("k", 0):
-                    nc.sync.dma_start(offsets[:], offs)
+        def load_planes(name, src, first, count):
+            planes = keep.tile([P, count, T], F32, name="%s_planes%d" % (name, first), tag="%s%d" % (name, first), align_bytes=64)
+            nc.sync.dma_start(out=planes[:], in_=src.rearrange("(p j) c -> p j c", j=PACK)[:, first:first + count, :])
+            for j in range(count):
+                pools[name, first + j] = planes[:, j, :]
 
-        load_pool("k", kT)
+        load_planes("k", kT, 0, 3)
+        nc.sync.dma_start(offsets[:], offs)
+        vectors = keep.tile([P, K_PASS], F32, name="vectors")
+        nc.gpsimd.memset(vectors[:], 0.0)
+        for i, src in enumerate((lse, delta, rw)):
+            nc.sync.dma_start(out=vectors[PASSES * i:PASSES * (i + 1), :], in_=src[0].rearrange("(g r) o -> g (r o)", g=PASSES))
+        load_planes("k", kT, 3, 1)
         q_raw = keep.tile([P, PACK, R], F32, name="q_raw", tag="q_then_p")
         nc.sync.dma_start(out=q_raw[:], in_=qT[0].rearrange("(p j) r -> p j r", j=PACK))
 
-        vectors = keep.tile([P, K_PASS], F32, name="vectors")
-        nc.vector.memset(vectors[:], 0.0)
-        for i, src in enumerate((lse, delta, rw)):
-            nc.scalar.dma_start(out=vectors[PASSES * i:PASSES * (i + 1), :], in_=src[0].rearrange("(g r) o -> g (r o)", g=PASSES))
         identity = keep.tile([P, P], F32, name="identity")
         make_identity(nc, identity[:])
         turned = ring.tile([P, PACK, P], F32, name="turned", tag="bank")
@@ -68,7 +71,8 @@ def tile_attend_gat_pl_lse_k_kernel(tc, qT, kT, vT, doT, lse, delta, rw, qm, off
         delta_rw = keep.tile([P, PACK, 2 * PASSES], F32, name="delta_rw")
         nc.vector.tensor_copy(out=delta_rw[:], in_=turned[:, :, PASSES:3 * PASSES])
 
-        load_pool("v", vT)
+        for first, count in ((0, 2), (2, 1), (3, 1)):
+            load_planes("v", vT, first, count)
         do_raw = {}
         for g in range(PASSES):
             for a in range(2):
@@ -83,24 +87,24 @@ def tile_attend_gat_pl_lse_k_kernel(tc, qT, kT, vT, doT, lse, delta, rw, qm, off
         windows = []
         for j in range(PACK):
             windows.append(keep.tile([P, T], F32, name="window%d" % j))
-            nc.vector.memset(windows[j][:], 0.0)
+            nc.gpsimd.memset(windows[j][:], 0.0)
 
         def deal(engine, name, raw, h):
-            dealt = keep.tile([P, 2, P, PACK], BF16, name=name + "_dealt", align_bytes=64)
+            dealt = keep.tile([P, 2, P, PACK], BF16, name=name + "_dealt", tag=name + "_dealt", align_bytes=64)
             move(engine, dealt[:].rearrange("p u s j -> p s j u"),
                  raw.rearrange("p j (s c) -> p s j c", c=PACK)[:, :, :, 2 * h:2 * h + 2])
             return dealt
 
-        def quantize(name, grouped, width, fmt):
-            codes = keep.tile([P, width], U32, name=name + "_codes", align_bytes=64)
+        def quantize(name, grouped, width, fmt, tag=None):
+            codes = keep.tile([P, width], U32, name=name + "_codes", tag=tag or name + "_codes", align_bytes=64)
             scales = keep.tile([P, width], U8, name=name + "_scales", align_bytes=64)
             for first in range(0, width, 2 * P):
                 nc.vector.quantize_mx(out=codes[:, first:first + 2 * P].bitcast(fmt), scales=scales[:, first:first + 2 * P],
                                       in_=grouped[:, PACK * first:PACK * (first + 2 * P)])
             return codes, scales, fmt
 
-        def quantize_dealt(name, dealt, fmt):
-            return quantize(name, dealt[:].rearrange("p u s j -> p (u s j)"), 2 * P, fmt)
+        def quantize_dealt(name, dealt, fmt, tag=None):
+            return quantize(name, dealt[:].rearrange("p u s j -> p (u s j)"), 2 * P, fmt, tag)
 
         def product(out, stationary, u, moving, start, stop):
             cols = slice(u * P, (u + 1) * P)
@@ -108,10 +112,10 @@ def tile_attend_gat_pl_lse_k_kernel(tc, qT, kT, vT, doT, lse, delta, rw, qm, off
                                 rhs=moving[0][:].bitcast(moving[2]), rhs_scale=moving[1][:], start=start, stop=stop)
 
         def gather(name, engines):
-            picked = keep.tile([P, PACK, N], F32, name=name + "_picked", tag="picked")
+            picked = keep.tile([P, PACK, N], F32, name=name + "_picked", tag="picked", align_bytes=64)
             for j in range(PACK):
-                nc.vector.tensor_copy(out=picked[:, j, :], in_=pools[name, j][:].indirect(offsets[:]))
-            grouped = keep.tile([P, N, PACK], BF16, name=name + "_grouped", align_bytes=64)
+                nc.vector.tensor_copy(out=picked[:, j, :], in_=pools[name, j].indirect(offsets[:]))
+            grouped = keep.tile([P, N, PACK], BF16, name=name + "_grouped", tag=name + "_grouped", align_bytes=64)
             for h in range(2):
                 cols = slice(h * N // 2, (h + 1) * N // 2)
                 move(engines[h], grouped[:, cols, :].rearrange("p (c i) j -> p c j i", i=4),
@@ -184,27 +188,33 @@ def tile_attend_gat_pl_lse_k_kernel(tc, qT, kT, vT, doT, lse, delta, rw, qm, off
                 nc.vector.quantize_mx(out=codes[:, cols].bitcast(E5M2), scales=scales[:, cols], in_=halves[h][:].rearrange("p n t -> p (n t)"))
             ds_mx[g] = codes, scales, E5M2
 
-        def prepare_qm(g, h, engine):
-            name = "qm%d%d" % (g, h)
-            qm_mx[g, h] = quantize_dealt(name, deal(engine, name, qm_raw[g][:], h), E4M3)
+        def deal_qm(g, h):
+            return deal("S", "qm%d%d" % (g, h), qm_raw[g][:], h)
+
+        def quantize_qm(g, h):
+            qm_mx[g, h] = quantize_dealt("qm%d%d" % (g, h), qm_dealt[g, h], E4M3, "qm10_dealt" if (g, h) == (0, 1) else None)
 
         prepare_do(0)
         prepare_do(1)
         form_ds(0, 1)
         form_ds(1, 2)
         quantize_ds(0, [regroup_ds(0, h, "G", ds_flat[0, 0][:, :, h * N // 2:(h + 1) * N // 2]) for h in range(2)])
-        prepare_qm(0, 0, "S")
+        qm_dealt = {}
+        for h in range(2):
+            qm_dealt[0, h] = deal_qm(0, h)
+        quantize_qm(0, 0)
         last_halves = [regroup_ds(1, h, "SV"[h], ds_flat[1, h][:]) for h in range(2)]
-        prepare_qm(1, 0, "S")
+        for h in range(2):
+            qm_dealt[1, h] = deal_qm(1, h)
         quantize_ds(1, last_halves)
-        prepare_qm(0, 1, "S")
-        prepare_qm(1, 1, "S")
+        for g, h in ((1, 0), (0, 1), (1, 1)):
+            quantize_qm(g, h)
 
         out_rows = out_0.rearrange("(p j) c -> p j c", j=PACK)
         dk_sb = keep.tile([P, T], F32, name="dk_sb", tag="k0", align_bytes=64)
         flat = []
         for half in range(2):
-            flat.append(keep.tile([P, PACK, T // 2], BF16, name="flat%d" % half, tag="v%d" % half, align_bytes=64))
+            flat.append(keep.tile([P, PACK, T // 2], BF16, name="flat%d" % half, tag=("v0", "picked")[half], align_bytes=64))
 
         def round_plane(engine, j, first, width):
             half, at = divmod(first, T // 2)
@@ -217,13 +227,12 @@ def tile_attend_gat_pl_lse_k_kernel(tc, qT, kT, vT, doT, lse, delta, rw, qm, off
             move("SSSS"[j], dk_sb[:, j * N:(j + 1) * N], dk[:])
             nc.vector.tensor_copy(out=windows[j][:].indirect(offsets[:]), in_=dk_sb[:, j * N:(j + 1) * N])
             nc.sync.dma_start(out=out_rows[:, j, :], in_=windows[j][:])
-        for j in (0, 1):
-            for half in (1, 0):
-                round_plane("S", j, half * 2 * CW, 2 * CW)
-        round_plane("V", 3, 2 * CW, 2 * CW)
-        round_plane("S", 2, 2 * CW, 2 * CW)
-        for j in (2, 3):
-            round_plane("V", j, 0, 2 * CW)
+        for j, half in ((0, 0), (0, 1), (1, 1)):
+            round_plane("G", j, half * 2 * CW, 2 * CW)
+        for j, half in ((1, 0), (2, 0), (2, 1)):
+            round_plane("S", j, half * 2 * CW, 2 * CW)
+        for half in (1, 0):
+            round_plane("V", 3, half * 2 * CW, 2 * CW)
 
         out_codes = keep.tile([P, T], U32, name="out_codes", tag="k3", align_bytes=64)
         out_scales = keep.tile([P, T], U8, name="out_scales", align_bytes=64)
@@ -237,7 +246,7 @@ def tile_attend_gat_pl_lse_k_kernel(tc, qT, kT, vT, doT, lse, delta, rw, qm, off
 
         grouped_out = {}
         for c in (2, 3, 0, 1):
-            grouped_out[c] = keep.tile([P, CW, PACK], BF16, name="grouped_out%d" % c, tag=("k1", "k2", "v2", "v3")[c], align_bytes=64)
+            grouped_out[c] = keep.tile([P, CW, PACK], BF16, name="grouped_out%d" % c, tag=("k_grouped", "v_grouped", "v2", "v3")[c], align_bytes=64)
             move("VVSS"[c], grouped_out[c][:].rearrange("p (c i) j -> p c j i", i=4),
                  flat[c // 2][:, :, (c % 2) * CW:(c % 2 + 1) * CW].rearrange("p j (c i) -> p c j i", i=4))
         for c in range(CHUNKS):

@@ -227,10 +227,10 @@ def tile_attend_gat_pl_lse_k_kernel(tc, qT, kT, vT, doT, lse, delta, rw, qm, off
             move("SSSS"[j], dk_sb[:, j * N:(j + 1) * N], dk[:])
             nc.vector.tensor_copy(out=windows[j][:].indirect(offsets[:]), in_=dk_sb[:, j * N:(j + 1) * N])
             nc.sync.dma_start(out=out_rows[:, j, :], in_=windows[j][:])
-        for j, half in ((0, 0), (0, 1), (1, 1)):
-            round_plane("G", j, half * 2 * CW, 2 * CW)
-        for j, half in ((1, 0), (2, 0), (2, 1)):
-            round_plane("S", j, half * 2 * CW, 2 * CW)
+        for j, first, width in ((0, 0, 2 * CW), (0, 2 * CW, 2 * CW), (1, 3 * CW, CW)):
+            round_plane("G", j, first, width)
+        for j, first, width in ((1, 0, 2 * CW), (1, 2 * CW, CW), (2, 0, 2 * CW), (2, 2 * CW, 2 * CW)):
+            round_plane("S", j, first, width)
         for half in (1, 0):
             round_plane("V", 3, half * 2 * CW, 2 * CW)
 
@@ -247,13 +247,31 @@ def tile_attend_gat_pl_lse_k_kernel(tc, qT, kT, vT, doT, lse, delta, rw, qm, off
         grouped_out = {}
         for c in (2, 3, 0, 1):
             grouped_out[c] = keep.tile([P, CW, PACK], BF16, name="grouped_out%d" % c, tag=("k_grouped", "v_grouped", "v2", "v3")[c], align_bytes=64)
-            move("VVSS"[c], grouped_out[c][:].rearrange("p (c i) j -> p c j i", i=4),
-                 flat[c // 2][:, :, (c % 2) * CW:(c % 2 + 1) * CW].rearrange("p j (c i) -> p c j i", i=4))
-        for c in range(CHUNKS):
+
+        def interleave(engine, c, first, width):
+            at = (c % 2) * CW + first
+            move(engine, grouped_out[c][:, first:first + width, :].rearrange("p (c i) j -> p c j i", i=4),
+                 flat[c // 2][:, :, at:at + width].rearrange("p j (c i) -> p c j i", i=4))
+
+        def quantize_chunk(c):
             cols = slice(c * CW, (c + 1) * CW)
             nc.vector.quantize_mx(out=out_codes[:, cols].bitcast(E4M3), scales=out_scales[:, cols],
                                   in_=grouped_out[c][:].rearrange("p n j -> p (n j)"))
-            if c >= 1:
-                stored = slice(0, 2 * CW) if c == 1 else cols
-                nc.sync.dma_start(out=words[:, stored], in_=out_codes[:, stored].bitcast(I32))
-        store_scales(0, T, (nc.scalar, nc.scalar, nc.scalar, nc.scalar))
+
+        def store_words(first, count):
+            cols = slice(first * CW, (first + count) * CW)
+            nc.sync.dma_start(out=words[:, cols], in_=out_codes[:, cols].bitcast(I32))
+
+        interleave("S", 2, 0, CW)
+        interleave("S", 3, 0, CW // 2)
+        for c in (0, 1):
+            interleave("V", c, 0, CW)
+        for c in (0, 1):
+            quantize_chunk(c)
+        store_words(0, 2)
+        quantize_chunk(2)
+        store_words(2, 1)
+        interleave("V", 3, CW // 2, CW // 2)
+        quantize_chunk(3)
+        store_words(3, 1)
+        store_scales(0, T, (nc.scalar, nc.sync, nc.scalar, nc.sync))

@@ -39,7 +39,9 @@ def tile_attend_gat_pl_lse_k_kernel(tc, qT, kT, vT, doT, lse, delta, rw, qm, off
     with ExitStack() as ctx:
         keep = ctx.enter_context(tc.tile_pool(name="keep", bufs=1))
         psum = ctx.enter_context(tc.psum_pool(name="psum", bufs=1))
-        ring = ctx.enter_context(tc.psum_pool(name="ring", bufs=4))
+
+        def bank(name, g, t):
+            return psum.tile([P, N], F32, name="%s%d%d" % (name, g, t), tag="bank%d%d" % (g, t))
 
         offsets = keep.tile([P, N // 16], U16, name="offsets")
 
@@ -63,7 +65,7 @@ def tile_attend_gat_pl_lse_k_kernel(tc, qT, kT, vT, doT, lse, delta, rw, qm, off
 
         identity = keep.tile([P, P], F32, name="identity")
         make_identity(nc, identity[:])
-        turned = ring.tile([P, PACK, P], F32, name="turned", tag="bank")
+        turned = psum.tile([P, PACK, P], F32, name="turned", tag="bank13")
         for t in range(PACK):
             nc.tensor.transpose(turned[:, t, :], vectors[:, t::PACK], identity[:])
         neg_lse = keep.tile([P, PACK, PASSES], F32, name="neg_lse")
@@ -89,8 +91,8 @@ def tile_attend_gat_pl_lse_k_kernel(tc, qT, kT, vT, doT, lse, delta, rw, qm, off
             windows.append(keep.tile([P, T], F32, name="window%d" % j))
             nc.gpsimd.memset(windows[j][:], 0.0)
 
-        def deal(engine, name, raw, h):
-            dealt = keep.tile([P, 2, P, PACK], BF16, name=name + "_dealt", tag=name + "_dealt", align_bytes=64)
+        def deal(engine, name, raw, h, tag=None):
+            dealt = keep.tile([P, 2, P, PACK], BF16, name=name + "_dealt", tag=tag or name + "_dealt", align_bytes=64)
             move(engine, dealt[:].rearrange("p u s j -> p s j u"),
                  raw.rearrange("p j (s c) -> p s j c", c=PACK)[:, :, :, 2 * h:2 * h + 2])
             return dealt
@@ -132,7 +134,7 @@ def tile_attend_gat_pl_lse_k_kernel(tc, qT, kT, vT, doT, lse, delta, rw, qm, off
         gated = keep.tile([P, PASSES * PACK, N], F32, name="gated", tag="q_then_p")
         for g in range(PASSES):
             for t in range(PACK):
-                scores = ring.tile([P, N], F32, name="scores", tag="bank")
+                scores = bank("scores", g, t)
                 product(scores[:], q_mx[g, t // 2], t % 2, k_mx, True, True)
                 mine = gated[:, g * PACK + t, :]
                 nc.scalar.activation(out=mine, in_=scores[:], func=ACT.Exp, bias=neg_lse[:, t, g:g + 1], scale=1.0)
@@ -153,86 +155,96 @@ def tile_attend_gat_pl_lse_k_kernel(tc, qT, kT, vT, doT, lse, delta, rw, qm, off
                 dealt.append(keep.tile([P, 2, P, PACK], BF16, name="do%d%d_dealt" % (g, h), tag="do%d%d" % (g, h), align_bytes=64))
             for a in range(2):
                 for h in range(2):
-                    move("S", dealt[h][:, :, a * P // 2:(a + 1) * P // 2, :].rearrange("p u s j -> p s j u"),
+                    move("V" if (g, a) == (1, 0) else "S", dealt[h][:, :, a * P // 2:(a + 1) * P // 2, :].rearrange("p u s j -> p s j u"),
                          do_raw[g, a][:].rearrange("p j (s c) -> p s j c", c=PACK)[:, :, :, 2 * h:2 * h + 2])
             for h in range(2):
                 do_mx[g, h] = quantize_dealt("do%d%d" % (g, h), dealt[h], E5M2)
 
-        def form_ds(g, parts):
+        def form_ds(g, widths, order):
             dp = []
             for t in range(PACK):
-                dp.append(ring.tile([P, N], F32, name="dp", tag="bank"))
+                dp.append(bank("dp", g, t))
                 product(dp[t][:], do_mx[g, t // 2], t % 2, v_mx, True, True)
-            width = N // parts
-            for h in range(parts):
-                cols = slice(h * width, (h + 1) * width)
-                ds_flat[g, h] = keep.tile([P, PACK, width], BF16, name="ds_flat%d%d" % (g, h))
-                for t in range(PACK):
-                    nc.vector.scalar_tensor_tensor(out=ds_flat[g, h][:, t, :], in0=dp[t][:, cols], scalar=delta_rw[:, t, g:g + 1],
-                                                   in1=gated[:, g * PACK + t, cols], op0=ALU.subtract, op1=ALU.mult)
+            for i, width in enumerate(widths):
+                ds_flat[g, i] = keep.tile([P, PACK, width], BF16, name="ds_flat%d%d" % (g, i), tag="ds_flat%d%d" % (g, i), align_bytes=64)
+            for i, t in order:
+                cols = slice(sum(widths[:i]), sum(widths[:i + 1]))
+                nc.vector.scalar_tensor_tensor(out=ds_flat[g, i][:, t, :], in0=dp[t][:, cols], scalar=delta_rw[:, t, g:g + 1],
+                                               in1=gated[:, g * PACK + t, cols], op0=ALU.subtract, op1=ALU.mult)
 
-        def regroup_ds(g, h, engine, flat_half):
-            grouped = keep.tile([P, N // 2, PACK], BF16, name="ds_grouped%d%d" % (g, h), tag="do%d%d" % (1 - g, 1 - h), align_bytes=64)
+        def regroup_ds(name, engine, flat_part, width, tag):
+            grouped = keep.tile([P, width, PACK], BF16, name=name, tag=tag, align_bytes=64)
             if engine == "G":
-                nc.gpsimd.tensor_scalar(out=grouped[:], in0=flat_half.rearrange("p t n -> p n t"),
+                nc.gpsimd.tensor_scalar(out=grouped[:], in0=flat_part.rearrange("p t n -> p n t"),
                                         scalar1=1.0, scalar2=0.0, op0=ALU.mult, op1=ALU.add)
             else:
-                move(engine, grouped[:].rearrange("p (c i) t -> p c t i", i=4), flat_half.rearrange("p t (c i) -> p c t i", i=4))
+                move(engine, grouped[:].rearrange("p (c i) t -> p c t i", i=4), flat_part.rearrange("p t (c i) -> p c t i", i=4))
             return grouped
 
-        def quantize_ds(g, halves):
-            codes = keep.tile([P, N], U32, name="ds%d_codes" % g, align_bytes=64)
-            scales = keep.tile([P, N], U8, name="ds%d_scales" % g, align_bytes=64)
-            for h in range(2):
-                cols = slice(h * N // 2, (h + 1) * N // 2)
-                nc.vector.quantize_mx(out=codes[:, cols].bitcast(E5M2), scales=scales[:, cols], in_=halves[h][:].rearrange("p n t -> p (n t)"))
-            ds_mx[g] = codes, scales, E5M2
+        for g in range(PASSES):
+            ds_mx[g] = (keep.tile([P, N], U32, name="ds%d_codes" % g, tag="ds%d_codes" % g, align_bytes=64),
+                        keep.tile([P, N], U8, name="ds%d_scales" % g, align_bytes=64), E5M2)
 
-        def deal_qm(g, h):
-            return deal("S", "qm%d%d" % (g, h), qm_raw[g][:], h)
+        def quantize_ds(g, first, width, grouped):
+            cols = slice(first, first + width)
+            nc.vector.quantize_mx(out=ds_mx[g][0][:, cols].bitcast(E5M2), scales=ds_mx[g][1][:, cols], in_=grouped[:].rearrange("p n t -> p (n t)"))
 
-        def quantize_qm(g, h):
-            qm_mx[g, h] = quantize_dealt("qm%d%d" % (g, h), qm_dealt[g, h], E4M3, "qm10_dealt" if (g, h) == (0, 1) else None)
+        def quantize_qm(g, h, first, count):
+            if (g, h) not in qm_mx:
+                qm_mx[g, h] = (keep.tile([P, 2 * P], U32, name="qm%d%d_codes" % (g, h), align_bytes=64),
+                               keep.tile([P, 2 * P], U8, name="qm%d%d_scales" % (g, h), align_bytes=64), E4M3)
+            cols = slice(first * P, (first + count) * P)
+            nc.vector.quantize_mx(out=qm_mx[g, h][0][:, cols].bitcast(E4M3), scales=qm_mx[g, h][1][:, cols],
+                                  in_=qm_dealt[g, h][:, first:first + count, :, :].rearrange("p u s j -> p (u s j)"))
 
+        last_widths = (N // 2, N // 4, N // 4)
+        last_firsts = (0, N // 2, 3 * N // 4)
         prepare_do(0)
         prepare_do(1)
-        form_ds(0, 1)
-        form_ds(1, 2)
-        quantize_ds(0, [regroup_ds(0, h, "G", ds_flat[0, 0][:, :, h * N // 2:(h + 1) * N // 2]) for h in range(2)])
+        form_ds(0, (N // 2, N // 2), ((0, 0), (1, 0), (0, 1), (1, 1), (0, 2), (0, 3), (1, 2), (1, 3)))
+        form_ds(1, last_widths, [(i, t) for i in range(3) for t in range(PACK)])
+        first_parts = [regroup_ds("ds_grouped0%d" % h, "SG"[h], ds_flat[0, h][:], N // 2, "do1%d" % h) for h in range(2)]
         qm_dealt = {}
+        qm_dealt[0, 0] = deal("S", "qm00", qm_raw[0][:], 0)
+        qm_dealt[1, 0] = deal("S", "qm10", qm_raw[1][:], 0)
+        last_parts = [regroup_ds("ds_grouped1%d" % i, "GSS"[i], ds_flat[1, i][:], last_widths[i], "ds_grouped1%d" % i) for i in range(3)]
         for h in range(2):
-            qm_dealt[0, h] = deal_qm(0, h)
-        quantize_qm(0, 0)
-        last_halves = [regroup_ds(1, h, "SV"[h], ds_flat[1, h][:]) for h in range(2)]
-        for h in range(2):
-            qm_dealt[1, h] = deal_qm(1, h)
-        quantize_ds(1, last_halves)
-        for g, h in ((1, 0), (0, 1), (1, 1)):
-            quantize_qm(g, h)
+            quantize_ds(0, h * N // 2, N // 2, first_parts[h])
+        quantize_qm(0, 0, 0, 1)
+        quantize_qm(1, 0, 0, 1)
+        quantize_ds(1, last_firsts[0], last_widths[0], last_parts[0])
+        for i in (1, 2):
+            quantize_ds(1, last_firsts[i], last_widths[i], last_parts[i])
+        qm_dealt[1, 1] = deal("S", "qm11", qm_raw[1][:], 1, "ds_flat12")
+        qm_dealt[0, 1] = deal("V", "qm01", qm_raw[0][:], 1, "ds_grouped12")
+        for g in range(PASSES):
+            quantize_qm(g, 0, 1, 1)
+        quantize_qm(1, 1, 0, 2)
+        quantize_qm(0, 1, 0, 2)
 
         out_rows = out_0.rearrange("(p j) c -> p j c", j=PACK)
         dk_sb = keep.tile([P, T], F32, name="dk_sb", tag="k0", align_bytes=64)
         flat = []
         for half in range(2):
-            flat.append(keep.tile([P, PACK, T // 2], BF16, name="flat%d" % half, tag=("v0", "picked")[half], align_bytes=64))
+            flat.append(keep.tile([P, PACK, T // 2], BF16, name="flat%d" % half, tag=("v0", "ds1_codes")[half], align_bytes=64))
 
         def round_plane(engine, j, first, width):
             half, at = divmod(first, T // 2)
             move(engine, flat[half][:, j, at:at + width], windows[j][:, first:first + width])
 
+        dk = [bank("dk", 0, j) for j in range(PACK)]
         for j in range(PACK):
-            dk = psum.tile([P, N], F32, name="dk%d" % j)
             for g in range(PASSES):
-                product(dk[:], qm_mx[g, j // 2], j % 2, ds_mx[g], g == 0, g == PASSES - 1)
-            move("SSSS"[j], dk_sb[:, j * N:(j + 1) * N], dk[:])
+                product(dk[j][:], qm_mx[g, j // 2], j % 2, ds_mx[g], g == 0, g == PASSES - 1)
+        for j in range(PACK):
+            move("S", dk_sb[:, j * N:(j + 1) * N], dk[j][:])
             nc.vector.tensor_copy(out=windows[j][:].indirect(offsets[:]), in_=dk_sb[:, j * N:(j + 1) * N])
             nc.sync.dma_start(out=out_rows[:, j, :], in_=windows[j][:])
-        for j, first, width in ((0, 0, 2 * CW), (0, 2 * CW, 2 * CW), (1, 3 * CW, CW)):
-            round_plane("G", j, first, width)
-        for j, first, width in ((1, 0, 2 * CW), (1, 2 * CW, CW), (2, 0, 2 * CW), (2, 2 * CW, 2 * CW)):
-            round_plane("S", j, first, width)
-        for half in (1, 0):
-            round_plane("V", 3, half * 2 * CW, 2 * CW)
+        for j in range(PACK - 1):
+            round_plane("G", j, 0, 2 * CW)
+            round_plane("S", j, 2 * CW, 2 * CW)
+        round_plane("V", 3, 0, 2 * CW)
+        round_plane("S", 3, 2 * CW, 2 * CW)
 
         out_codes = keep.tile([P, T], U32, name="out_codes", tag="k3", align_bytes=64)
         out_scales = keep.tile([P, T], U8, name="out_scales", align_bytes=64)
@@ -269,9 +281,9 @@ def tile_attend_gat_pl_lse_k_kernel(tc, qT, kT, vT, doT, lse, delta, rw, qm, off
         for c in (0, 1):
             quantize_chunk(c)
         store_words(0, 2)
+        interleave("V", 3, CW // 2, CW // 2)
         quantize_chunk(2)
         store_words(2, 1)
-        interleave("V", 3, CW // 2, CW // 2)
         quantize_chunk(3)
         store_words(3, 1)
         store_scales(0, T, (nc.scalar, nc.sync, nc.scalar, nc.sync))

@@ -155,7 +155,7 @@ def tile_attend_gat_pl_lse_k_kernel(tc, qT, kT, vT, doT, lse, delta, rw, qm, off
                 dealt.append(keep.tile([P, 2, P, PACK], BF16, name="do%d%d_dealt" % (g, h), tag="do%d%d" % (g, h), align_bytes=64))
             for a in range(2):
                 for h in range(2):
-                    move("V" if (g, a) == (1, 0) else "S", dealt[h][:, :, a * P // 2:(a + 1) * P // 2, :].rearrange("p u s j -> p s j u"),
+                    move(["SSSS","VVSS"][g][2 * a + h], dealt[h][:, :, a * P // 2:(a + 1) * P // 2, :].rearrange("p u s j -> p s j u"),
                          do_raw[g, a][:].rearrange("p j (s c) -> p s j c", c=PACK)[:, :, :, 2 * h:2 * h + 2])
             for h in range(2):
                 do_mx[g, h] = quantize_dealt("do%d%d" % (g, h), dealt[h], E5M2)
@@ -206,13 +206,13 @@ def tile_attend_gat_pl_lse_k_kernel(tc, qT, kT, vT, doT, lse, delta, rw, qm, off
         first_parts = [regroup_ds("ds_grouped0%d" % h, "SG"[h], ds_flat[0, h][:], N // 2, "do1%d" % h) for h in range(2)]
         qm_dealt = {}
         qm_dealt[0, 0] = deal("S", "qm00", qm_raw[0][:], 0)
-        qm_dealt[1, 0] = deal("S", "qm10", qm_raw[1][:], 0)
-        last_parts = [regroup_ds("ds_grouped1%d" % i, "GSS"[i], ds_flat[1, i][:], last_widths[i], "ds_grouped1%d" % i) for i in range(3)]
+        last_parts = [regroup_ds("ds_grouped1%d" % i, "SSS"[i], ds_flat[1, i][:], last_widths[i], "ds_grouped1%d" % i) for i in range(3)]
         for h in range(2):
             quantize_ds(0, h * N // 2, N // 2, first_parts[h])
         quantize_qm(0, 0, 0, 1)
-        quantize_qm(1, 0, 0, 1)
+        qm_dealt[1, 0] = deal("V", "qm10", qm_raw[1][:], 0)
         quantize_ds(1, last_firsts[0], last_widths[0], last_parts[0])
+        quantize_qm(1, 0, 0, 1)
         for i in (1, 2):
             quantize_ds(1, last_firsts[i], last_widths[i], last_parts[i])
         qm_dealt[1, 1] = deal("S", "qm11", qm_raw[1][:], 1, "ds_flat12")

@@ -124,6 +124,25 @@ def tile_attend_gat_pl_lse_k_kernel(tc, qT, kT, vT, doT, lse, delta, rw, qm, off
                      picked[:, :, cols].rearrange("p j (c i) -> p c j i", i=4))
             return quantize(name, grouped[:].rearrange("p n j -> p (n j)"), N, E4M3)
 
+        def gather_values():
+            picked = keep.tile([P, PACK, N], F32, name="v_picked", tag="picked", align_bytes=64)
+            grouped = keep.tile([P, N, PACK], BF16, name="v_grouped", tag="v_grouped", align_bytes=64)
+
+            def pair(first, cols):
+                move("V", grouped[:, cols, first:first + 2].rearrange("p (c i) j -> p c j i", i=4),
+                     picked[:, first:first + 2, cols].rearrange("p j (c i) -> p c j i", i=4))
+
+            for j in range(PACK - 1):
+                nc.vector.tensor_copy(out=picked[:, j, :], in_=pools["v", j].indirect(offsets[:]))
+                if j == 1:
+                    pair(0, slice(0, N))
+            halves = [slice(h * N // 2, (h + 1) * N // 2) for h in range(2)]
+            for h in range(2):
+                nc.vector.tensor_copy(out=picked[:, PACK - 1, halves[h]], in_=pools["v", PACK - 1].indirect(offsets[:, h * N // 32:(h + 1) * N // 32]))
+            for h in range(2):
+                pair(2, halves[h])
+            return quantize("v", grouped[:].rearrange("p n j -> p (n j)"), N, E4M3)
+
         k_mx = gather("k", "VV")
         q_mx = {}
         for g in range(PASSES):
@@ -139,10 +158,10 @@ def tile_attend_gat_pl_lse_k_kernel(tc, qT, kT, vT, doT, lse, delta, rw, qm, off
                 mine = gated[:, g * PACK + t, :]
                 nc.scalar.activation(out=mine, in_=scores[:], func=ACT.Exp, bias=neg_lse[:, t, g:g + 1], scale=1.0)
                 if g == 0:
-                    nc.vector.tensor_scalar(out=mine, in0=mine, scalar1=delta_rw[:, t, PASSES + g:PASSES + g + 1], scalar2=None, op0=ALU.mult)
+                    nc.gpsimd.tensor_scalar(out=mine, in0=mine, scalar1=delta_rw[:, t, PASSES + g:PASSES + g + 1], scalar2=-0.0, op0=ALU.mult, op1=ALU.add)
                 else:
                     nc.scalar.activation(out=mine, in_=mine, func=ACT.Copy, scale=delta_rw[:, t, PASSES + g:PASSES + g + 1])
-        v_mx = gather("v", "VV")
+        v_mx = gather_values()
 
         do_mx = {}
         ds_flat = {}
@@ -155,7 +174,7 @@ def tile_attend_gat_pl_lse_k_kernel(tc, qT, kT, vT, doT, lse, delta, rw, qm, off
                 dealt.append(keep.tile([P, 2, P, PACK], BF16, name="do%d%d_dealt" % (g, h), tag="do%d%d" % (g, h), align_bytes=64))
             for a in range(2):
                 for h in range(2):
-                    move(["SSSS","VVSS"][g][2 * a + h], dealt[h][:, :, a * P // 2:(a + 1) * P // 2, :].rearrange("p u s j -> p s j u"),
+                    move(["SSVS","VVSS"][g][2 * a + h], dealt[h][:, :, a * P // 2:(a + 1) * P // 2, :].rearrange("p u s j -> p s j u"),
                          do_raw[g, a][:].rearrange("p j (s c) -> p s j c", c=PACK)[:, :, :, 2 * h:2 * h + 2])
             for h in range(2):
                 do_mx[g, h] = quantize_dealt("do%d%d" % (g, h), dealt[h], E5M2)
@@ -240,21 +259,19 @@ def tile_attend_gat_pl_lse_k_kernel(tc, qT, kT, vT, doT, lse, delta, rw, qm, off
             move("S", dk_sb[:, j * N:(j + 1) * N], dk[j][:])
             nc.vector.tensor_copy(out=windows[j][:].indirect(offsets[:]), in_=dk_sb[:, j * N:(j + 1) * N])
             nc.sync.dma_start(out=out_rows[:, j, :], in_=windows[j][:])
-        for j in range(PACK - 1):
-            round_plane("G", j, 0, 2 * CW)
-            round_plane("S", j, 2 * CW, 2 * CW)
-        round_plane("V", 3, 0, 2 * CW)
-        round_plane("S", 3, 2 * CW, 2 * CW)
+        for j in range(PACK):
+            for half in range(2):
+                round_plane(("GS", "GS", "SS", "VV")[j][half], j, half * 2 * CW, 2 * CW)
 
         out_codes = keep.tile([P, T], U32, name="out_codes", tag="k3", align_bytes=64)
-        out_scales = keep.tile([P, T], U8, name="out_scales", align_bytes=64)
+        out_scales = keep.tile([P, CW], U8, name="out_scales", align_bytes=64)
         words = out_1[0].rearrange("p c l -> p (c l)").bitcast(I32)
         scale_rows = out_2[0].bitcast(I32)
 
-        def store_scales(first, width, queues):
+        def store_scales(queues):
             for quad in range(4):
-                queues[quad].dma_start(out=scale_rows[4 * quad:4 * quad + 4, first // 4:(first + width) // 4],
-                                       in_=out_scales[32 * quad:32 * quad + 4, first:first + width].bitcast(I32))
+                queues[quad].dma_start(out=scale_rows[4 * quad:4 * quad + 4, :].rearrange("f (c w) -> c f w", c=CHUNKS),
+                                       in_=out_scales[32 * quad:32 * quad + 4 * CHUNKS, :].bitcast(I32))
 
         grouped_out = {}
         for c in (2, 3, 0, 1):
@@ -267,7 +284,7 @@ def tile_attend_gat_pl_lse_k_kernel(tc, qT, kT, vT, doT, lse, delta, rw, qm, off
 
         def quantize_chunk(c):
             cols = slice(c * CW, (c + 1) * CW)
-            nc.vector.quantize_mx(out=out_codes[:, cols].bitcast(E4M3), scales=out_scales[:, cols],
+            nc.vector.quantize_mx(out=out_codes[:, cols].bitcast(E4M3), scales=out_scales[4 * c:P, :],
                                   in_=grouped_out[c][:].rearrange("p n j -> p (n j)"))
 
         def store_words(first, count):
@@ -286,4 +303,4 @@ def tile_attend_gat_pl_lse_k_kernel(tc, qT, kT, vT, doT, lse, delta, rw, qm, off
         store_words(2, 1)
         quantize_chunk(3)
         store_words(3, 1)
-        store_scales(0, T, (nc.scalar, nc.sync, nc.scalar, nc.sync))
+        store_scales((nc.scalar, nc.sync, nc.scalar, nc.sync))

@@ -73,7 +73,7 @@ def tile_attend_gat_pl_lse_k_kernel(tc, qT, kT, vT, doT, lse, delta, rw, qm, off
         delta_rw = keep.tile([P, PACK, 2 * PASSES], F32, name="delta_rw")
         nc.vector.tensor_copy(out=delta_rw[:], in_=turned[:, :, PASSES:3 * PASSES])
 
-        for first, count in ((0, 2), (2, 1), (3, 1)):
+        for first, count in ((0, 1), (1, 1), (2, 1), (3, 1)):
             load_planes("v", vT, first, count)
         do_raw = {}
         for g in range(PASSES):
@@ -157,7 +157,9 @@ def tile_attend_gat_pl_lse_k_kernel(tc, qT, kT, vT, doT, lse, delta, rw, qm, off
                 product(scores[:], q_mx[g, t // 2], t % 2, k_mx, True, True)
                 mine = gated[:, g * PACK + t, :]
                 nc.scalar.activation(out=mine, in_=scores[:], func=ACT.Exp, bias=neg_lse[:, t, g:g + 1], scale=1.0)
-                if g == 0:
+                if g == 0 and t >= 2:
+                    nc.vector.tensor_scalar(out=mine, in0=mine, scalar1=delta_rw[:, t, PASSES + g:PASSES + g + 1], scalar2=None, op0=ALU.mult)
+                elif g == 0:
                     nc.gpsimd.tensor_scalar(out=mine, in0=mine, scalar1=delta_rw[:, t, PASSES + g:PASSES + g + 1], scalar2=-0.0, op0=ALU.mult, op1=ALU.add)
                 else:
                     nc.scalar.activation(out=mine, in_=mine, func=ACT.Copy, scale=delta_rw[:, t, PASSES + g:PASSES + g + 1])
@@ -174,8 +176,11 @@ def tile_attend_gat_pl_lse_k_kernel(tc, qT, kT, vT, doT, lse, delta, rw, qm, off
                 dealt.append(keep.tile([P, 2, P, PACK], BF16, name="do%d%d_dealt" % (g, h), tag="do%d%d" % (g, h), align_bytes=64))
             for a in range(2):
                 for h in range(2):
-                    move(["SSVS","VVSS"][g][2 * a + h], dealt[h][:, :, a * P // 2:(a + 1) * P // 2, :].rearrange("p u s j -> p s j u"),
-                         do_raw[g, a][:].rearrange("p j (s c) -> p s j c", c=PACK)[:, :, :, 2 * h:2 * h + 2])
+                    engines = (("S", "S", "SV", "S"), ("V", "V", "S", "S"))[g][2 * a + h]
+                    rows = P // 2 // len(engines)
+                    for i, engine in enumerate(engines):
+                        move(engine, dealt[h][:, :, a * P // 2 + i * rows:a * P // 2 + (i + 1) * rows, :].rearrange("p u s j -> p s j u"),
+                             do_raw[g, a][:].rearrange("p j (s c) -> p s j c", c=PACK)[:, i * rows:(i + 1) * rows, :, 2 * h:2 * h + 2])
             for h in range(2):
                 do_mx[g, h] = quantize_dealt("do%d%d" % (g, h), dealt[h], E5M2)
 
@@ -292,15 +297,14 @@ def tile_attend_gat_pl_lse_k_kernel(tc, qT, kT, vT, doT, lse, delta, rw, qm, off
             nc.sync.dma_start(out=words[:, cols], in_=out_codes[:, cols].bitcast(I32))
 
         interleave("S", 2, 0, CW)
-        interleave("S", 3, 0, CW // 2)
+        interleave("S", 3, 0, 3 * CW // 4)
         for c in (0, 1):
             interleave("V", c, 0, CW)
         for c in (0, 1):
             quantize_chunk(c)
         store_words(0, 2)
-        interleave("V", 3, CW // 2, CW // 2)
-        quantize_chunk(2)
-        store_words(2, 1)
-        quantize_chunk(3)
-        store_words(3, 1)
+        interleave("V", 3, 3 * CW // 4, CW // 4)
+        for c in (2, 3):
+            quantize_chunk(c)
+            store_words(c, 1)
         store_scales((nc.scalar, nc.sync, nc.scalar, nc.sync))

@@ -233,18 +233,22 @@ def tile_attend_gat_pl_lse_k_kernel(tc, qT, kT, vT, doT, lse, delta, rw, qm, off
         last_parts = [regroup_ds("ds_grouped1%d" % i, "SSS"[i], ds_flat[1, i][:], last_widths[i], "ds_grouped1%d" % i) for i in range(3)]
         for h in range(2):
             quantize_ds(0, h * N // 2, N // 2, first_parts[h])
-        quantize_qm(0, 0, 0, 1)
+        for u in range(2):
+            quantize_qm(0, 0, u, 1)
         qm_dealt[1, 0] = deal("V", "qm10", qm_raw[1][:], 0)
         quantize_ds(1, last_firsts[0], last_widths[0], last_parts[0])
         quantize_qm(1, 0, 0, 1)
         for i in (1, 2):
             quantize_ds(1, last_firsts[i], last_widths[i], last_parts[i])
-        qm_dealt[1, 1] = deal("S", "qm11", qm_raw[1][:], 1, "ds_flat12")
         qm_dealt[0, 1] = deal("V", "qm01", qm_raw[0][:], 1, "ds_grouped12")
-        for g in range(PASSES):
-            quantize_qm(g, 0, 1, 1)
-        quantize_qm(1, 1, 0, 2)
-        quantize_qm(0, 1, 0, 2)
+        qm_dealt[1, 1] = keep.tile([P, 2, P, PACK], BF16, name="qm11_dealt", tag="ds_flat12", align_bytes=64)
+        for engine, rows in (("S", slice(0, 3 * P // 4)), ("V", slice(3 * P // 4, P))):
+            move(engine, qm_dealt[1, 1][:, :, rows, :].rearrange("p u s j -> p s j u"),
+                 qm_raw[1][:].rearrange("p j (s c) -> p s j c", c=PACK)[:, rows, :, 2:4])
+        quantize_qm(1, 0, 1, 1)
+        for u in range(2):
+            for g in range(PASSES):
+                quantize_qm(g, 1, u, 1)
 
         out_rows = out_0.rearrange("(p j) c -> p j c", j=PACK)
         dk_sb = keep.tile([P, T], F32, name="dk_sb", tag="k0", align_bytes=64)
@@ -296,14 +300,16 @@ def tile_attend_gat_pl_lse_k_kernel(tc, qT, kT, vT, doT, lse, delta, rw, qm, off
             cols = slice(first * CW, (first + count) * CW)
             nc.sync.dma_start(out=words[:, cols], in_=out_codes[:, cols].bitcast(I32))
 
+        share = 5 * CW // 8
+        piece = (CW - share) // 2
         interleave("S", 2, 0, CW)
-        interleave("S", 3, 0, 3 * CW // 4)
+        interleave("S", 3, 0, share)
         for c in (0, 1):
             interleave("V", c, 0, CW)
         for c in (0, 1):
             quantize_chunk(c)
+            interleave("V", 3, share + c * piece, piece)
         store_words(0, 2)
-        interleave("V", 3, 3 * CW // 4, CW // 4)
         for c in (2, 3):
             quantize_chunk(c)
             store_words(c, 1)

@@ -300,16 +300,14 @@ def tile_attend_gat_pl_lse_k_kernel(tc, qT, kT, vT, doT, lse, delta, rw, qm, off
             cols = slice(first * CW, (first + count) * CW)
             nc.sync.dma_start(out=words[:, cols], in_=out_codes[:, cols].bitcast(I32))
 
-        share = 5 * CW // 8
-        piece = (CW - share) // 2
         interleave("S", 2, 0, CW)
-        interleave("S", 3, 0, share)
+        interleave("S", 3, 0, 3 * CW // 4)
         for c in (0, 1):
             interleave("V", c, 0, CW)
         for c in (0, 1):
             quantize_chunk(c)
-            interleave("V", 3, share + c * piece, piece)
         store_words(0, 2)
+        interleave("V", 3, 3 * CW // 4, CW // 4)
         for c in (2, 3):
             quantize_chunk(c)
             store_words(c, 1)

@@ -227,6 +227,8 @@ def tile_attend_gat_pl_lse_k_kernel(tc, qT, kT, vT, doT, lse, delta, rw, qm, off
         prepare_do(1)
         form_ds(0, (N // 2, N // 2), ((0, 0), (1, 0), (0, 1), (1, 1), (0, 2), (0, 3), (1, 2), (1, 3)))
         form_ds(1, last_widths, [(i, t) for i in range(3) for t in range(PACK)])
+        for t in range(2):
+            product(bank("warm", 1, t)[:], q_mx[0, 0], t, k_mx, True, True)
         first_parts = [regroup_ds("ds_grouped0%d" % h, "SG"[h], ds_flat[0, h][:], N // 2, "do1%d" % h) for h in range(2)]
         qm_dealt = {}
         qm_dealt[0, 0] = deal("S", "qm00", qm_raw[0][:], 0)

@@ -293,24 +293,27 @@ def tile_attend_gat_pl_lse_k_kernel(tc, qT, kT, vT, doT, lse, delta, rw, qm, off
             move(engine, grouped_out[c][:, first:first + width, :].rearrange("p (c i) j -> p c j i", i=4),
                  flat[c // 2][:, :, at:at + width].rearrange("p j (c i) -> p c j i", i=4))
 
-        def quantize_chunk(c):
-            cols = slice(c * CW, (c + 1) * CW)
-            nc.vector.quantize_mx(out=out_codes[:, cols].bitcast(E4M3), scales=out_scales[4 * c:P, :],
-                                  in_=grouped_out[c][:].rearrange("p n j -> p (n j)"))
+        def quantize_chunk(c, first, width):
+            cols = slice(c * CW + first, c * CW + first + width)
+            nc.vector.quantize_mx(out=out_codes[:, cols].bitcast(E4M3), scales=out_scales[4 * c:P, first:first + width],
+                                  in_=grouped_out[c][:, first:first + width, :].rearrange("p n j -> p (n j)"))
 
-        def store_words(first, count):
-            cols = slice(first * CW, (first + count) * CW)
+        def store_words(first, width):
+            cols = slice(first, first + width)
             nc.sync.dma_start(out=words[:, cols], in_=out_codes[:, cols].bitcast(I32))
 
         interleave("S", 2, 0, CW)
-        interleave("S", 3, 0, 3 * CW // 4)
+        interleave("S", 3, 0, CW // 2)
+        interleave("S", 3, CW // 2, CW // 4)
         for c in (0, 1):
             interleave("V", c, 0, CW)
         for c in (0, 1):
-            quantize_chunk(c)
-        store_words(0, 2)
+            for first in (0, CW // 2):
+                quantize_chunk(c, first, CW // 2)
+        store_words(0, 2 * CW)
         interleave("V", 3, 3 * CW // 4, CW // 4)
         for c in (2, 3):
-            quantize_chunk(c)
-            store_words(c, 1)
+            for first in (0, CW // 2):
+                quantize_chunk(c, first, CW // 2)
+            store_words(c * CW, CW)
         store_scales((nc.scalar, nc.sync, nc.scalar, nc.sync))

@@ -23,6 +23,9 @@ K_PASS = P * PACK
 PASSES = R // K_PASS
 CHUNKS = 4
 CW = T // CHUNKS
+SCAT = "VVSS"
+ROUND = (("V",0,0,1024),("V",0,1024,1024),("V",1,0,1024),("V",1,1024,1024),("V",2,1024,1024),("S",3,1024,1024),("V",2,0,1024),("V",3,0,1024))
+EARLY = (("S",2,0,512),("S",3,0,256),("S",3,256,256),("V",0,0,512),("V",1,0,512))
 
 
 def tile_attend_gat_pl_lse_k_kernel(tc, qT, kT, vT, doT, lse, delta, rw, qm, offs, out_0, out_1, out_2):
@@ -268,11 +271,15 @@ def tile_attend_gat_pl_lse_k_kernel(tc, qT, kT, vT, doT, lse, delta, rw, qm, off
                 product(dk[j][:], qm_mx[g, j // 2], j % 2, ds_mx[g], g == 0, g == PASSES - 1)
         for j in range(PACK):
             move("S", dk_sb[:, j * N:(j + 1) * N], dk[j][:])
-            nc.vector.tensor_copy(out=windows[j][:].indirect(offsets[:]), in_=dk_sb[:, j * N:(j + 1) * N])
+            if SCAT[j] == "V":
+                nc.vector.tensor_copy(out=windows[j][:].indirect(offsets[:]), in_=dk_sb[:, j * N:(j + 1) * N])
+            else:
+                for h in range(2):
+                    nc.scalar.activation(out=windows[j][:].indirect(offsets[:, h * N // 32:(h + 1) * N // 32]),
+                                         in_=dk_sb[:, j * N + h * N // 2:j * N + (h + 1) * N // 2], func=ACT.Copy)
             nc.sync.dma_start(out=out_rows[:, j, :], in_=windows[j][:])
-        for j in range(PACK):
-            for half in range(2):
-                round_plane(("GS", "GS", "SS", "VV")[j][half], j, half * 2 * CW, 2 * CW)
+        for engine, j, first, width in ROUND:
+            round_plane(engine, j, first, width)
 
         out_codes = keep.tile([P, T], U32, name="out_codes", tag="k3", align_bytes=64)
         out_scales = keep.tile([P, CW], U8, name="out_scales", align_bytes=64)
@@ -302,16 +309,12 @@ def tile_attend_gat_pl_lse_k_kernel(tc, qT, kT, vT, doT, lse, delta, rw, qm, off
             cols = slice(first, first + width)
             nc.sync.dma_start(out=words[:, cols], in_=out_codes[:, cols].bitcast(I32))
 
-        interleave("S", 2, 0, CW)
-        interleave("S", 3, 0, CW // 2)
-        interleave("S", 3, CW // 2, CW // 4)
-        for c in (0, 1):
-            interleave("V", c, 0, CW)
+        for engine, c, first, width in EARLY:
+            interleave(engine, c, first, width)
         for c in (0, 1):
             for first in (0, CW // 2):
                 quantize_chunk(c, first, CW // 2)
         store_words(0, 2 * CW)
-        interleave("V", 3, 3 * CW // 4, CW // 4)
         for c in (2, 3):
             for first in (0, CW // 2):
                 quantize_chunk(c, first, CW // 2)

@@ -23,8 +23,8 @@ K_PASS = P * PACK
 PASSES = R // K_PASS
 CHUNKS = 4
 CW = T // CHUNKS
-SCAT = "VVSS"
-ROUND = (("V",0,0,1024),("V",0,1024,1024),("V",1,0,1024),("V",1,1024,1024),("V",2,1024,1024),("S",3,1024,1024),("V",2,0,1024),("V",3,0,1024))
+SCAT = "VVVS"
+ROUND = (("V",0,1024,1024),("V",1,1024,1024),("V",2,1024,1024),("S",3,1024,1024),("V",0,0,1024),("V",1,0,1024),("V",2,0,1024),("V",3,0,1024))
 EARLY = (("S",2,0,512),("S",3,0,256),("S",3,256,256),("V",0,0,512),("V",1,0,512))
 
 
@@ -100,21 +100,21 @@ def tile_attend_gat_pl_lse_k_kernel(tc, qT, kT, vT, doT, lse, delta, rw, qm, off
                  raw.rearrange("p j (s c) -> p s j c", c=PACK)[:, :, :, 2 * h:2 * h + 2])
             return dealt
 
-        def quantize(name, grouped, width, fmt, tag=None):
+        def quantize(name, grouped, width, fmt, tag=None, step=2 * P):
             codes = keep.tile([P, width], U32, name=name + "_codes", tag=tag or name + "_codes", align_bytes=64)
             scales = keep.tile([P, width], U8, name=name + "_scales", align_bytes=64)
-            for first in range(0, width, 2 * P):
-                nc.vector.quantize_mx(out=codes[:, first:first + 2 * P].bitcast(fmt), scales=scales[:, first:first + 2 * P],
-                                      in_=grouped[:, PACK * first:PACK * (first + 2 * P)])
+            for first in range(0, width, step):
+                nc.vector.quantize_mx(out=codes[:, first:first + step].bitcast(fmt), scales=scales[:, first:first + step],
+                                      in_=grouped[:, PACK * first:PACK * (first + step)])
             return codes, scales, fmt
 
-        def quantize_dealt(name, dealt, fmt, tag=None):
-            return quantize(name, dealt[:].rearrange("p u s j -> p (u s j)"), 2 * P, fmt, tag)
+        def quantize_dealt(name, dealt, fmt, step=2 * P):
+            return quantize(name, dealt[:].rearrange("p u s j -> p (u s j)"), 2 * P, fmt, None, step)
 
-        def product(out, stationary, u, moving, start, stop):
+        def product(out, stationary, u, moving, start, stop, slots=slice(0, N)):
             cols = slice(u * P, (u + 1) * P)
             nc.tensor.matmul_mx(out=out, lhsT=stationary[0][:, cols].bitcast(stationary[2]), lhsT_scale=stationary[1][:, cols],
-                                rhs=moving[0][:].bitcast(moving[2]), rhs_scale=moving[1][:], start=start, stop=stop)
+                                rhs=moving[0][:, slots].bitcast(moving[2]), rhs_scale=moving[1][:, slots], start=start, stop=stop)
 
         def gather(name, engines):
             picked = keep.tile([P, PACK, N], F32, name=name + "_picked", tag="picked", align_bytes=64)
@@ -179,24 +179,26 @@ def tile_attend_gat_pl_lse_k_kernel(tc, qT, kT, vT, doT, lse, delta, rw, qm, off
                 dealt.append(keep.tile([P, 2, P, PACK], BF16, name="do%d%d_dealt" % (g, h), tag="do%d%d" % (g, h), align_bytes=64))
             for a in range(2):
                 for h in range(2):
-                    engines = (("S", "S", "SV", "S"), ("V", "V", "S", "S"))[g][2 * a + h]
+                    engines = (("S", "S", "SV", "S"), ("S", "S", "S", "S"))[g][2 * a + h]
                     rows = P // 2 // len(engines)
                     for i, engine in enumerate(engines):
                         move(engine, dealt[h][:, :, a * P // 2 + i * rows:a * P // 2 + (i + 1) * rows, :].rearrange("p u s j -> p s j u"),
                              do_raw[g, a][:].rearrange("p j (s c) -> p s j c", c=PACK)[:, i * rows:(i + 1) * rows, :, 2 * h:2 * h + 2])
             for h in range(2):
-                do_mx[g, h] = quantize_dealt("do%d%d" % (g, h), dealt[h], E5M2)
+                do_mx[g, h] = quantize_dealt("do%d%d" % (g, h), dealt[h], E5M2, P if (g, h) == (0, 0) else 2 * P)
 
         def form_ds(g, widths, order):
-            dp = []
-            for t in range(PACK):
-                dp.append(bank("dp", g, t))
-                product(dp[t][:], do_mx[g, t // 2], t % 2, v_mx, True, True)
+            span = N // 2
+            dp = {}
             for i, width in enumerate(widths):
                 ds_flat[g, i] = keep.tile([P, PACK, width], BF16, name="ds_flat%d%d" % (g, i), tag="ds_flat%d%d" % (g, i), align_bytes=64)
             for i, t in order:
                 cols = slice(sum(widths[:i]), sum(widths[:i + 1]))
-                nc.vector.scalar_tensor_tensor(out=ds_flat[g, i][:, t, :], in0=dp[t][:, cols], scalar=delta_rw[:, t, g:g + 1],
+                part, at = divmod(cols.start, span)
+                if (part, t) not in dp:
+                    dp[part, t] = psum.tile([P, span], F32, name="dp%d%d%d" % (g, part, t), tag="bank%d%d" % (g, t))
+                    product(dp[part, t][:], do_mx[g, t // 2], t % 2, v_mx, True, True, slice(part * span, (part + 1) * span))
+                nc.vector.scalar_tensor_tensor(out=ds_flat[g, i][:, t, :], in0=dp[part, t][:, at:at + widths[i]], scalar=delta_rw[:, t, g:g + 1],
                                                in1=gated[:, g * PACK + t, cols], op0=ALU.subtract, op1=ALU.mult)
 
         def regroup_ds(name, engine, flat_part, width, tag):
@@ -216,47 +218,47 @@ def tile_attend_gat_pl_lse_k_kernel(tc, qT, kT, vT, doT, lse, delta, rw, qm, off
             cols = slice(first, first + width)
             nc.vector.quantize_mx(out=ds_mx[g][0][:, cols].bitcast(E5M2), scales=ds_mx[g][1][:, cols], in_=grouped[:].rearrange("p n t -> p (n t)"))
 
-        def quantize_qm(g, h, first, count):
-            if (g, h) not in qm_mx:
-                qm_mx[g, h] = (keep.tile([P, 2 * P], U32, name="qm%d%d_codes" % (g, h), align_bytes=64),
-                               keep.tile([P, 2 * P], U8, name="qm%d%d_scales" % (g, h), align_bytes=64), E4M3)
-            cols = slice(first * P, (first + count) * P)
-            nc.vector.quantize_mx(out=qm_mx[g, h][0][:, cols].bitcast(E4M3), scales=qm_mx[g, h][1][:, cols],
-                                  in_=qm_dealt[g, h][:, first:first + count, :, :].rearrange("p u s j -> p (u s j)"))
+        def quantize_qm(g, j):
+            later = min(j, 1)
+            if later not in qm_mx:
+                width = (1, PACK - 1)[later] * PASSES * P
+                qm_mx[later] = (keep.tile([P, width], U32, name="qm_codes%d" % later, tag="qm_codes", align_bytes=64),
+                                keep.tile([P, width], U8, name="qm_scales%d" % later, tag="qm_scales%d" % later, align_bytes=64), E4M3)
+            place = (j - later) * PASSES + g
+            cols = slice(place * P, (place + 1) * P)
+            nc.vector.quantize_mx(out=qm_mx[later][0][:, cols].bitcast(E4M3), scales=qm_mx[later][1][:, cols],
+                                  in_=qm_dealt[g, j // 2][:, j % 2, :, :].rearrange("p s j -> p (s j)"))
 
         last_widths = (N // 2, N // 4, N // 4)
         last_firsts = (0, N // 2, 3 * N // 4)
         prepare_do(0)
         prepare_do(1)
-        form_ds(0, (N // 2, N // 2), ((0, 0), (1, 0), (0, 1), (1, 1), (0, 2), (0, 3), (1, 2), (1, 3)))
+        form_ds(0, (N // 2, N // 2), [(i, t) for i in range(2) for t in range(PACK)])
         form_ds(1, last_widths, [(i, t) for i in range(3) for t in range(PACK)])
         for t in range(2):
             product(bank("warm", 1, t)[:], q_mx[0, 0], t, k_mx, True, True)
         first_parts = [regroup_ds("ds_grouped0%d" % h, "SG"[h], ds_flat[0, h][:], N // 2, "do1%d" % h) for h in range(2)]
         qm_dealt = {}
         qm_dealt[0, 0] = deal("S", "qm00", qm_raw[0][:], 0)
-        last_parts = [regroup_ds("ds_grouped1%d" % i, "SSS"[i], ds_flat[1, i][:], last_widths[i], "ds_grouped1%d" % i) for i in range(3)]
+        first_half = keep.tile([P, N // 2, PACK], BF16, name="ds_grouped10", align_bytes=64)
+        nc.gpsimd.tensor_scalar(out=first_half[:, :P, :], in0=ds_flat[1, 0][:, :, :P].rearrange("p t n -> p n t"),
+                                scalar1=1.0, scalar2=0.0, op0=ALU.mult, op1=ALU.add)
+        move("S", first_half[:, P:, :].rearrange("p (c i) t -> p c t i", i=4), ds_flat[1, 0][:, :, P:].rearrange("p t (c i) -> p c t i", i=4))
+        last_parts = [first_half] + [regroup_ds("ds_grouped1%d" % i, "S", ds_flat[1, i][:], last_widths[i], "ds_grouped1%d" % i) for i in (1, 2)]
         for h in range(2):
             quantize_ds(0, h * N // 2, N // 2, first_parts[h])
-        for u in range(2):
-            quantize_qm(0, 0, u, 1)
-        qm_dealt[1, 0] = deal("V", "qm10", qm_raw[1][:], 0)
+        quantize_qm(0, 0)
         quantize_ds(1, last_firsts[0], last_widths[0], last_parts[0])
-        quantize_qm(1, 0, 0, 1)
+        dealt_row = keep.tile([P, 3 * K_PASS], BF16, name="dealt_row", align_bytes=64)
+        qm_dealt[1, 0] = dealt_row[:, K_PASS:].rearrange("p (u s j) -> p u s j", u=2, j=PACK)
+        for engine, rows in (("V", slice(0, P // 2)), ("S", slice(P // 2, P))):
+            move(engine, qm_dealt[1, 0][:, :, rows, :].rearrange("p u s j -> p s j u"),
+                 qm_raw[1][:].rearrange("p j (s c) -> p s j c", c=PACK)[:, rows, :, 0:2])
         for i in (1, 2):
             quantize_ds(1, last_firsts[i], last_widths[i], last_parts[i])
-        qm_dealt[0, 1] = deal("V", "qm01", qm_raw[0][:], 1, "ds_grouped12")
-        qm_dealt[1, 1] = keep.tile([P, 2, P, PACK], BF16, name="qm11_dealt", tag="ds_flat12", align_bytes=64)
-        for engine, rows in (("S", slice(0, 3 * P // 4)), ("V", slice(3 * P // 4, P))):
-            move(engine, qm_dealt[1, 1][:, :, rows, :].rearrange("p u s j -> p s j u"),
-                 qm_raw[1][:].rearrange("p j (s c) -> p s j c", c=PACK)[:, rows, :, 2:4])
-        quantize_qm(1, 0, 1, 1)
-        for u in range(2):
-            for g in range(PASSES):
-                quantize_qm(g, 1, u, 1)
+        quantize_qm(1, 0)
 
         out_rows = out_0.rearrange("(p j) c -> p j c", j=PACK)
-        dk_sb = keep.tile([P, T], F32, name="dk_sb", tag="k0", align_bytes=64)
         flat = []
         for half in range(2):
             flat.append(keep.tile([P, PACK, T // 2], BF16, name="flat%d" % half, tag=("v0", "ds1_codes")[half], align_bytes=64))
@@ -265,19 +267,41 @@ def tile_attend_gat_pl_lse_k_kernel(tc, qT, kT, vT, doT, lse, delta, rw, qm, off
             half, at = divmod(first, T // 2)
             move(engine, flat[half][:, j, at:at + width], windows[j][:, first:first + width])
 
-        dk = [bank("dk", 0, j) for j in range(PACK)]
+        dk = [None] + [bank("dk", 0, j) for j in range(1, PACK)]
+        dk_halves = [psum.tile([P, N // 2], F32, name="dk_half%d" % h, tag=("bank00", "bank12")[h]) for h in range(2)]
+        for h in range(2):
+            product(dk_halves[h][:], qm_mx[0], 0, ds_mx[0], True, False, slice(h * N // 2, (h + 1) * N // 2))
+        for i in range(3):
+            h, at = divmod(last_firsts[i], N // 2)
+            product(dk_halves[h][:, at:at + last_widths[i]], qm_mx[0], 1, ds_mx[1], False, i != 1,
+                    slice(last_firsts[i], last_firsts[i] + last_widths[i]))
         for j in range(PACK):
-            for g in range(PASSES):
-                product(dk[j][:], qm_mx[g, j // 2], j % 2, ds_mx[g], g == 0, g == PASSES - 1)
-        for j in range(PACK):
-            move("S", dk_sb[:, j * N:(j + 1) * N], dk[j][:])
+            dk_sb = keep.tile([P, N], F32, name="dk_sb%d" % j, tag=("k0", "do_raw01", "v1", "do_raw00")[j], align_bytes=64)
+            if j == 0:
+                for h in range(2):
+                    move("S", dk_sb[:, h * N // 2:(h + 1) * N // 2], dk_halves[h][:])
+            else:
+                move("S", dk_sb[:], dk[j][:])
             if SCAT[j] == "V":
-                nc.vector.tensor_copy(out=windows[j][:].indirect(offsets[:]), in_=dk_sb[:, j * N:(j + 1) * N])
+                nc.vector.tensor_copy(out=windows[j][:].indirect(offsets[:]), in_=dk_sb[:])
             else:
                 for h in range(2):
                     nc.scalar.activation(out=windows[j][:].indirect(offsets[:, h * N // 32:(h + 1) * N // 32]),
-                                         in_=dk_sb[:, j * N + h * N // 2:j * N + (h + 1) * N // 2], func=ACT.Copy)
+                                         in_=dk_sb[:, h * N // 2:(h + 1) * N // 2], func=ACT.Copy)
             nc.sync.dma_start(out=out_rows[:, j, :], in_=windows[j][:])
+            if j == 0:
+                for g in range(PASSES):
+                    quantize_qm(g, 1)
+                for g in range(PASSES):
+                    row = keep.tile([P, 2 * K_PASS], BF16, name="last_pair", tag="qm_scales0", align_bytes=64) if g else dealt_row
+                    qm_dealt[g, 1] = row[:, :2 * K_PASS].rearrange("p (u s j) -> p u s j", u=2, j=PACK)
+                    move("VS"[g], qm_dealt[g, 1].rearrange("p u s j -> p s j u"), qm_raw[g][:].rearrange("p j (s c) -> p s j c", c=PACK)[:, :, :, 2:4])
+                for u in range(2):
+                    for g in range(PASSES):
+                        quantize_qm(g, 2 + u)
+                for jj in range(1, PACK):
+                    for g in range(PASSES):
+                        product(dk[jj][:], qm_mx[1], (jj - 1) * PASSES + g, ds_mx[g], g == 0, g == PASSES - 1)
         for engine, j, first, width in ROUND:
             round_plane(engine, j, first, width)
 

@@ -23,9 +23,9 @@ K_PASS = P * PACK
 PASSES = R // K_PASS
 CHUNKS = 4
 CW = T // CHUNKS
-SCAT = "VVVS"
-ROUND = (("V",0,1024,1024),("V",1,1024,1024),("V",2,1024,1024),("S",3,1024,1024),("V",0,0,1024),("V",1,0,1024),("V",2,0,1024),("V",3,0,1024))
-EARLY = (("S",2,0,512),("S",3,0,256),("S",3,256,256),("V",0,0,512),("V",1,0,512))
+SCAT = "VSSS"
+ROUND = (("V",0,0,1024),("V",0,1024,1024),("V",1,0,1024),("V",1,1024,1024),("V",2,0,1024),("S",2,1536,512),("S",3,1536,512),("V",3,0,1024),("V",2,1024,512),("V",3,1024,512))
+EARLY = (("S",0,0,512),("S",1,0,512),("V",2,0,512),("V",3,0,256),("S",3,256,256))
 
 
 def tile_attend_gat_pl_lse_k_kernel(tc, qT, kT, vT, doT, lse, delta, rw, qm, offs, out_0, out_1, out_2):
@@ -257,15 +257,21 @@ def tile_attend_gat_pl_lse_k_kernel(tc, qT, kT, vT, doT, lse, delta, rw, qm, off
         for i in (1, 2):
             quantize_ds(1, last_firsts[i], last_widths[i], last_parts[i])
         quantize_qm(1, 0)
+        qm_dealt[0, 1] = dealt_row[:, :2 * K_PASS].rearrange("p (u s j) -> p u s j", u=2, j=PACK)
+        move("V", qm_dealt[0, 1].rearrange("p u s j -> p s j u"), qm_raw[0][:].rearrange("p j (s c) -> p s j c", c=PACK)[:, :, :, 2:4])
+        qm_dealt[1, 1] = keep.tile([P, 2, P, PACK], BF16, name="qm11_dealt", tag="ds_flat12", align_bytes=64)
+        for engine, rows in (("S", slice(0, 3 * P // 4)), ("V", slice(3 * P // 4, P))):
+            move(engine, qm_dealt[1, 1][:, :, rows, :].rearrange("p u s j -> p s j u"),
+                 qm_raw[1][:].rearrange("p j (s c) -> p s j c", c=PACK)[:, rows, :, 2:4])
 
         out_rows = out_0.rearrange("(p j) c -> p j c", j=PACK)
         flat = []
         for half in range(2):
-            flat.append(keep.tile([P, PACK, T // 2], BF16, name="flat%d" % half, tag=("v0", "ds1_codes")[half], align_bytes=64))
+            flat.append(keep.tile([P, 2, T // 2, 2], BF16, name="flat%d" % half, tag=("v0", "ds1_codes")[half], align_bytes=64))
 
         def round_plane(engine, j, first, width):
             half, at = divmod(first, T // 2)
-            move(engine, flat[half][:, j, at:at + width], windows[j][:, first:first + width])
+            move(engine, flat[half][:, j // 2, at:at + width, j % 2], windows[j][:, first:first + width])
 
         dk = [None] + [bank("dk", 0, j) for j in range(1, PACK)]
         dk_halves = [psum.tile([P, N // 2], F32, name="dk_half%d" % h, tag=("bank00", "bank12")[h]) for h in range(2)]
@@ -292,10 +298,6 @@ def tile_attend_gat_pl_lse_k_kernel(tc, qT, kT, vT, doT, lse, delta, rw, qm, off
             if j == 0:
                 for g in range(PASSES):
                     quantize_qm(g, 1)
-                for g in range(PASSES):
-                    row = keep.tile([P, 2 * K_PASS], BF16, name="last_pair", tag="qm_scales0", align_bytes=64) if g else dealt_row
-                    qm_dealt[g, 1] = row[:, :2 * K_PASS].rearrange("p (u s j) -> p u s j", u=2, j=PACK)
-                    move("VS"[g], qm_dealt[g, 1].rearrange("p u s j -> p s j u"), qm_raw[g][:].rearrange("p j (s c) -> p s j c", c=PACK)[:, :, :, 2:4])
                 for u in range(2):
                     for g in range(PASSES):
                         quantize_qm(g, 2 + u)
@@ -321,8 +323,10 @@ def tile_attend_gat_pl_lse_k_kernel(tc, qT, kT, vT, doT, lse, delta, rw, qm, off
 
         def interleave(engine, c, first, width):
             at = (c % 2) * CW + first
-            move(engine, grouped_out[c][:, first:first + width, :].rearrange("p (c i) j -> p c j i", i=4),
-                 flat[c // 2][:, :, at:at + width].rearrange("p j (c i) -> p c j i", i=4))
+            word = I32 if engine == "V" else U32
+            pairs = flat[c // 2][:].rearrange("p q n e -> p q (n e)").bitcast(word)
+            move(engine, grouped_out[c][:].bitcast(word)[:, first:first + width, :].rearrange("p (c i) q -> p c q i", i=4),
+                 pairs[:, :, at:at + width].rearrange("p q (c i) -> p c q i", i=4))
 
         def quantize_chunk(c, first, width):
             cols = slice(c * CW + first, c * CW + first + width)
@@ -335,12 +339,9 @@ def tile_attend_gat_pl_lse_k_kernel(tc, qT, kT, vT, doT, lse, delta, rw, qm, off
 
         for engine, c, first, width in EARLY:
             interleave(engine, c, first, width)
-        for c in (0, 1):
-            for first in (0, CW // 2):
-                quantize_chunk(c, first, CW // 2)
-        store_words(0, 2 * CW)
-        for c in (2, 3):
-            for first in (0, CW // 2):
-                quantize_chunk(c, first, CW // 2)
-            store_words(c * CW, CW)
+        for chunks in ((2,), (0, 1), (3,)):
+            for c in chunks:
+                for first in (0, CW // 2):
+                    quantize_chunk(c, first, CW // 2)
+            store_words(chunks[0] * CW, len(chunks) * CW)
         store_scales((nc.scalar, nc.sync, nc.scalar, nc.sync))

@@ -219,12 +219,12 @@ def tile_attend_gat_pl_lse_k_kernel(tc, qT, kT, vT, doT, lse, delta, rw, qm, off
             nc.vector.quantize_mx(out=ds_mx[g][0][:, cols].bitcast(E5M2), scales=ds_mx[g][1][:, cols], in_=grouped[:].rearrange("p n t -> p (n t)"))
 
         def quantize_qm(g, j):
-            later = min(j, 1)
+            later = j // 2
             if later not in qm_mx:
-                width = (1, PACK - 1)[later] * PASSES * P
-                qm_mx[later] = (keep.tile([P, width], U32, name="qm_codes%d" % later, tag="qm_codes", align_bytes=64),
+                width = 2 * PASSES * P
+                qm_mx[later] = (keep.tile([P, width], U32, name="qm_codes%d" % later, align_bytes=64),
                                 keep.tile([P, width], U8, name="qm_scales%d" % later, tag="qm_scales%d" % later, align_bytes=64), E4M3)
-            place = (j - later) * PASSES + g
+            place = j % 2 * PASSES + g
             cols = slice(place * P, (place + 1) * P)
             nc.vector.quantize_mx(out=qm_mx[later][0][:, cols].bitcast(E4M3), scales=qm_mx[later][1][:, cols],
                                   in_=qm_dealt[g, j // 2][:, j % 2, :, :].rearrange("p s j -> p (s j)"))
@@ -247,7 +247,8 @@ def tile_attend_gat_pl_lse_k_kernel(tc, qT, kT, vT, doT, lse, delta, rw, qm, off
         last_parts = [first_half] + [regroup_ds("ds_grouped1%d" % i, "S", ds_flat[1, i][:], last_widths[i], "ds_grouped1%d" % i) for i in (1, 2)]
         for h in range(2):
             quantize_ds(0, h * N // 2, N // 2, first_parts[h])
-        quantize_qm(0, 0)
+        for j in range(2):
+            quantize_qm(0, j)
         quantize_ds(1, last_firsts[0], last_widths[0], last_parts[0])
         dealt_row = keep.tile([P, 3 * K_PASS], BF16, name="dealt_row", align_bytes=64)
         qm_dealt[1, 0] = dealt_row[:, K_PASS:].rearrange("p (u s j) -> p u s j", u=2, j=PACK)
@@ -256,7 +257,8 @@ def tile_attend_gat_pl_lse_k_kernel(tc, qT, kT, vT, doT, lse, delta, rw, qm, off
                  qm_raw[1][:].rearrange("p j (s c) -> p s j c", c=PACK)[:, rows, :, 0:2])
         for i in (1, 2):
             quantize_ds(1, last_firsts[i], last_widths[i], last_parts[i])
-        quantize_qm(1, 0)
+        for j in range(2):
+            quantize_qm(1, j)
         qm_dealt[0, 1] = dealt_row[:, :2 * K_PASS].rearrange("p (u s j) -> p u s j", u=2, j=PACK)
         move("V", qm_dealt[0, 1].rearrange("p u s j -> p s j u"), qm_raw[0][:].rearrange("p j (s c) -> p s j c", c=PACK)[:, :, :, 2:4])
         qm_dealt[1, 1] = keep.tile([P, 2, P, PACK], BF16, name="qm11_dealt", tag="ds_flat12", align_bytes=64)
@@ -296,14 +298,12 @@ def tile_attend_gat_pl_lse_k_kernel(tc, qT, kT, vT, doT, lse, delta, rw, qm, off
                                          in_=dk_sb[:, h * N // 2:(h + 1) * N // 2], func=ACT.Copy)
             nc.sync.dma_start(out=out_rows[:, j, :], in_=windows[j][:])
             if j == 0:
-                for g in range(PASSES):
-                    quantize_qm(g, 1)
                 for u in range(2):
                     for g in range(PASSES):
                         quantize_qm(g, 2 + u)
                 for jj in range(1, PACK):
                     for g in range(PASSES):
-                        product(dk[jj][:], qm_mx[1], (jj - 1) * PASSES + g, ds_mx[g], g == 0, g == PASSES - 1)
+                        product(dk[jj][:], qm_mx[jj // 2], jj % 2 * PASSES + g, ds_mx[g], g == 0, g == PASSES - 1)
         for engine, j, first, width in ROUND:
             round_plane(engine, j, first, width)
 

@@ -61,7 +61,7 @@ def tile_attend_gat_pl_lse_k_kernel(tc, qT, kT, vT, doT, lse, delta, rw, qm, off
         vectors = keep.tile([P, K_PASS], F32, name="vectors")
         nc.gpsimd.memset(vectors[:], 0.0)
         for i, src in enumerate((lse, delta, rw)):
-            nc.sync.dma_start(out=vectors[PASSES * i:PASSES * (i + 1), :], in_=src[0].rearrange("(g r) o -> g (r o)", g=PASSES))
+            nc.scalar.dma_start(out=vectors[PASSES * i:PASSES * (i + 1), :], in_=src[0].rearrange("(g r) o -> g (r o)", g=PASSES))
         load_planes("k", kT, 3, 1)
         q_raw = keep.tile([P, PACK, R], F32, name="q_raw", tag="q_then_p")
         nc.sync.dma_start(out=q_raw[:], in_=qT[0].rearrange("(p j) r -> p j r", j=PACK))
@@ -339,9 +339,9 @@ def tile_attend_gat_pl_lse_k_kernel(tc, qT, kT, vT, doT, lse, delta, rw, qm, off
 
         for engine, c, first, width in EARLY:
             interleave(engine, c, first, width)
-        for chunks in ((2,), (0, 1), (3,)):
+        for chunks in ((2,), (0,), (1,), (3,)):
             for c in chunks:
                 for first in (0, CW // 2):
                     quantize_chunk(c, first, CW // 2)
             store_words(chunks[0] * CW, len(chunks) * CW)
-        store_scales((nc.scalar, nc.sync, nc.scalar, nc.sync))
+        store_scales((nc.scalar, nc.scalar, nc.scalar, nc.scalar))

@@ -235,8 +235,6 @@ def tile_attend_gat_pl_lse_k_kernel(tc, qT, kT, vT, doT, lse, delta, rw, qm, off
         prepare_do(1)
         form_ds(0, (N // 2, N // 2), [(i, t) for i in range(2) for t in range(PACK)])
         form_ds(1, last_widths, [(i, t) for i in range(3) for t in range(PACK)])
-        for t in range(2):
-            product(bank("warm", 1, t)[:], q_mx[0, 0], t, k_mx, True, True)
         first_parts = [regroup_ds("ds_grouped0%d" % h, "SG"[h], ds_flat[0, h][:], N // 2, "do1%d" % h) for h in range(2)]
         qm_dealt = {}
         qm_dealt[0, 0] = deal("S", "qm00", qm_raw[0][:], 0)

from contextlib import ExitStack

import concourse.mybir as mybir
from concourse.masks import make_identity

N, T, D, DV, R = 512, 2048, 512, 512, 1024
FLOPS = 2 * R * N * (D + DV + D)

F32 = mybir.dt.float32
BF16 = mybir.dt.bfloat16
I32 = mybir.dt.int32
U32 = mybir.dt.uint32
U16 = mybir.dt.uint16
U8 = mybir.dt.uint8
E4M3 = mybir.dt.float8_e4m3fn_x4
E5M2 = mybir.dt.float8_e5m2_x4
ACT = mybir.ActivationFunctionType
ALU = mybir.AluOpType

P = 128
PACK = 4
K_PASS = P * PACK
PASSES = R // K_PASS
CHUNKS = 4
CW = T // CHUNKS
SCAT = "VSSS"
ROUND = (("V",0,0,1024),("V",0,1024,1024),("V",1,0,1024),("V",1,1024,1024),("V",2,0,1024),("S",2,1536,512),("S",3,1536,512),("V",3,0,1024),("V",2,1024,512),("V",3,1024,512))
EARLY = (("S",0,0,512),("S",1,0,512),("V",2,0,512),("V",3,0,256),("S",3,256,256))


def tile_attend_gat_pl_lse_k_kernel(tc, qT, kT, vT, doT, lse, delta, rw, qm, offs, out_0, out_1, out_2):
    nc = tc.nc

    def move(engine, out, in_):
        if engine == "V":
            nc.vector.tensor_copy(out=out, in_=in_)
        elif engine == "G":
            nc.gpsimd.tensor_scalar(out=out, in0=in_, scalar1=1.0, scalar2=-0.0, op0=ALU.mult, op1=ALU.add)
        else:
            nc.scalar.copy(out=out, in_=in_)

    with ExitStack() as ctx:
        keep = ctx.enter_context(tc.tile_pool(name="keep", bufs=1))
        psum = ctx.enter_context(tc.psum_pool(name="psum", bufs=1))

        def bank(name, g, t):
            return psum.tile([P, N], F32, name="%s%d%d" % (name, g, t), tag="bank%d%d" % (g, t))

        offsets = keep.tile([P, N // 16], U16, name="offsets")

        pools = {}

        def load_planes(name, src, first, count):
            planes = keep.tile([P, count, T], F32, name="%s_planes%d" % (name, first), tag="%s%d" % (name, first), align_bytes=64)
            nc.sync.dma_start(out=planes[:], in_=src.rearrange("(p j) c -> p j c", j=PACK)[:, first:first + count, :])
            for j in range(count):
                pools[name, first + j] = planes[:, j, :]

        load_planes("k", kT, 0, 3)
        nc.sync.dma_start(offsets[:], offs)
        vectors = keep.tile([P, K_PASS], F32, name="vectors")
        nc.gpsimd.memset(vectors[:], 0.0)
        for i, src in enumerate((lse, delta, rw)):
            nc.scalar.dma_start(out=vectors[PASSES * i:PASSES * (i + 1), :], in_=src[0].rearrange("(g r) o -> g (r o)", g=PASSES))
        load_planes("k", kT, 3, 1)
        q_raw = keep.tile([P, PACK, R], F32, name="q_raw", tag="q_then_p")
        nc.sync.dma_start(out=q_raw[:], in_=qT[0].rearrange("(p j) r -> p j r", j=PACK))

        identity = keep.tile([P, P], F32, name="identity")
        make_identity(nc, identity[:])
        turned = psum.tile([P, PACK, P], F32, name="turned", tag="bank13")
        for t in range(PACK):
            nc.tensor.transpose(turned[:, t, :], vectors[:, t::PACK], identity[:])
        neg_lse = keep.tile([P, PACK, PASSES], F32, name="neg_lse")
        nc.vector.tensor_scalar(out=neg_lse[:], in0=turned[:, :, 0:PASSES], scalar1=-1.0, scalar2=None, op0=ALU.mult)
        delta_rw = keep.tile([P, PACK, 2 * PASSES], F32, name="delta_rw")
        nc.vector.tensor_copy(out=delta_rw[:], in_=turned[:, :, PASSES:3 * PASSES])

        for first, count in ((0, 1), (1, 1), (2, 1), (3, 1)):
            load_planes("v", vT, first, count)
        do_raw = {}
        for g in range(PASSES):
            for a in range(2):
                first = g * K_PASS + a * K_PASS // 2
                do_raw[g, a] = keep.tile([P, PACK, K_PASS // 2], F32, name="do_raw%d%d" % (g, a), align_bytes=64)
                nc.sync.dma_start(out=do_raw[g, a][:], in_=doT[0].rearrange("(p j) r -> p j r", j=PACK)[:, :, first:first + K_PASS // 2])
        qm_raw = []
        for g in range(PASSES):
            qm_raw.append(keep.tile([P, PACK, D], F32, name="qm_raw%d" % g))
            nc.sync.dma_start(out=qm_raw[g][:], in_=qm[0, g * K_PASS:(g + 1) * K_PASS, :].rearrange("(p t) d -> p t d", t=PACK))

        windows = []
        for j in range(PACK):
            windows.append(keep.tile([P, T], F32, name="window%d" % j))
            nc.gpsimd.memset(windows[j][:], 0.0)

        def deal(engine, name, raw, h, tag=None):
            dealt = keep.tile([P, 2, P, PACK], BF16, name=name + "_dealt", tag=tag or name + "_dealt", align_bytes=64)
            move(engine, dealt[:].rearrange("p u s j -> p s j u"),
                 raw.rearrange("p j (s c) -> p s j c", c=PACK)[:, :, :, 2 * h:2 * h + 2])
            return dealt

        def quantize(name, grouped, width, fmt, tag=None, step=2 * P):
            codes = keep.tile([P, width], U32, name=name + "_codes", tag=tag or name + "_codes", align_bytes=64)
            scales = keep.tile([P, width], U8, name=name + "_scales", align_bytes=64)
            for first in range(0, width, step):
                nc.vector.quantize_mx(out=codes[:, first:first + step].bitcast(fmt), scales=scales[:, first:first + step],
                                      in_=grouped[:, PACK * first:PACK * (first + step)])
            return codes, scales, fmt

        def quantize_dealt(name, dealt, fmt, step=2 * P):
            return quantize(name, dealt[:].rearrange("p u s j -> p (u s j)"), 2 * P, fmt, None, step)

        def product(out, stationary, u, moving, start, stop, slots=slice(0, N)):
            cols = slice(u * P, (u + 1) * P)
            nc.tensor.matmul_mx(out=out, lhsT=stationary[0][:, cols].bitcast(stationary[2]), lhsT_scale=stationary[1][:, cols],
                                rhs=moving[0][:, slots].bitcast(moving[2]), rhs_scale=moving[1][:, slots], start=start, stop=stop)

        def gather(name, engines):
            picked = keep.tile([P, PACK, N], F32, name=name + "_picked", tag="picked", align_bytes=64)
            for j in range(PACK):
                nc.vector.tensor_copy(out=picked[:, j, :], in_=pools[name, j].indirect(offsets[:]))
            grouped = keep.tile([P, N, PACK], BF16, name=name + "_grouped", tag=name + "_grouped", align_bytes=64)
            for h in range(2):
                cols = slice(h * N // 2, (h + 1) * N // 2)
                move(engines[h], grouped[:, cols, :].rearrange("p (c i) j -> p c j i", i=4),
                     picked[:, :, cols].rearrange("p j (c i) -> p c j i", i=4))
            return quantize(name, grouped[:].rearrange("p n j -> p (n j)"), N, E4M3)

        def gather_values():
            picked = keep.tile([P, PACK, N], F32, name="v_picked", tag="picked", align_bytes=64)
            grouped = keep.tile([P, N, PACK], BF16, name="v_grouped", tag="v_grouped", align_bytes=64)

            def pair(first, cols):
                move("V", grouped[:, cols, first:first + 2].rearrange("p (c i) j -> p c j i", i=4),
                     picked[:, first:first + 2, cols].rearrange("p j (c i) -> p c j i", i=4))

            for j in range(PACK - 1):
                nc.vector.tensor_copy(out=picked[:, j, :], in_=pools["v", j].indirect(offsets[:]))
                if j == 1:
                    pair(0, slice(0, N))
            halves = [slice(h * N // 2, (h + 1) * N // 2) for h in range(2)]
            for h in range(2):
                nc.vector.tensor_copy(out=picked[:, PACK - 1, halves[h]], in_=pools["v", PACK - 1].indirect(offsets[:, h * N // 32:(h + 1) * N // 32]))
            for h in range(2):
                pair(2, halves[h])
            return quantize("v", grouped[:].rearrange("p n j -> p (n j)"), N, E4M3)

        k_mx = gather("k", "VV")
        q_mx = {}
        for g in range(PASSES):
            for h in range(2):
                name = "q%d%d" % (g, h)
                q_mx[g, h] = quantize_dealt(name, deal("VVVS"[2 * g + h], name, q_raw[:, :, g * K_PASS:(g + 1) * K_PASS], h), E4M3)

        gated = keep.tile([P, PASSES * PACK, N], F32, name="gated", tag="q_then_p")
        for g in range(PASSES):
            for t in range(PACK):
                scores = bank("scores", g, t)
                product(scores[:], q_mx[g, t // 2], t % 2, k_mx, True, True)
                mine = gated[:, g * PACK + t, :]
                nc.scalar.activation(out=mine, in_=scores[:], func=ACT.Exp, bias=neg_lse[:, t, g:g + 1], scale=1.0)
                if g == 0 and t >= 2:
                    nc.vector.tensor_scalar(out=mine, in0=mine, scalar1=delta_rw[:, t, PASSES + g:PASSES + g + 1], scalar2=None, op0=ALU.mult)
                elif g == 0:
                    nc.gpsimd.tensor_scalar(out=mine, in0=mine, scalar1=delta_rw[:, t, PASSES + g:PASSES + g + 1], scalar2=-0.0, op0=ALU.mult, op1=ALU.add)
                else:
                    nc.scalar.activation(out=mine, in_=mine, func=ACT.Copy, scale=delta_rw[:, t, PASSES + g:PASSES + g + 1])
        v_mx = gather_values()

        do_mx = {}
        ds_flat = {}
        ds_mx = {}
        qm_mx = {}

        def prepare_do(g):
            dealt = []
            for h in range(2):
                dealt.append(keep.tile([P, 2, P, PACK], BF16, name="do%d%d_dealt" % (g, h), tag="do%d%d" % (g, h), align_bytes=64))
            for a in range(2):
                for h in range(2):
                    engines = (("S", "S", "SV", "S"), ("S", "S", "S", "S"))[g][2 * a + h]
                    rows = P // 2 // len(engines)
                    for i, engine in enumerate(engines):
                        move(engine, dealt[h][:, :, a * P // 2 + i * rows:a * P // 2 + (i + 1) * rows, :].rearrange("p u s j -> p s j u"),
                             do_raw[g, a][:].rearrange("p j (s c) -> p s j c", c=PACK)[:, i * rows:(i + 1) * rows, :, 2 * h:2 * h + 2])
            for h in range(2):
                do_mx[g, h] = quantize_dealt("do%d%d" % (g, h), dealt[h], E5M2, P if (g, h) == (0, 0) else 2 * P)

        def form_ds(g, widths, order):
            span = N // 2
            dp = {}
            for i, width in enumerate(widths):
                ds_flat[g, i] = keep.tile([P, PACK, width], BF16, name="ds_flat%d%d" % (g, i), tag="ds_flat%d%d" % (g, i), align_bytes=64)
            for i, t in order:
                cols = slice(sum(widths[:i]), sum(widths[:i + 1]))
                part, at = divmod(cols.start, span)
                if (part, t) not in dp:
                    dp[part, t] = psum.tile([P, span], F32, name="dp%d%d%d" % (g, part, t), tag="bank%d%d" % (g, t))
                    product(dp[part, t][:], do_mx[g, t // 2], t % 2, v_mx, True, True, slice(part * span, (part + 1) * span))
                nc.vector.scalar_tensor_tensor(out=ds_flat[g, i][:, t, :], in0=dp[part, t][:, at:at + widths[i]], scalar=delta_rw[:, t, g:g + 1],
                                               in1=gated[:, g * PACK + t, cols], op0=ALU.subtract, op1=ALU.mult)

        def regroup_ds(name, engine, flat_part, width, tag):
            grouped = keep.tile([P, width, PACK], BF16, name=name, tag=tag, align_bytes=64)
            if engine == "G":
                nc.gpsimd.tensor_scalar(out=grouped[:], in0=flat_part.rearrange("p t n -> p n t"),
                                        scalar1=1.0, scalar2=0.0, op0=ALU.mult, op1=ALU.add)
            else:
                move(engine, grouped[:].rearrange("p (c i) t -> p c t i", i=4), flat_part.rearrange("p t (c i) -> p c t i", i=4))
            return grouped

        for g in range(PASSES):
            ds_mx[g] = (keep.tile([P, N], U32, name="ds%d_codes" % g, tag="ds%d_codes" % g, align_bytes=64),
                        keep.tile([P, N], U8, name="ds%d_scales" % g, align_bytes=64), E5M2)

        def quantize_ds(g, first, width, grouped):
            cols = slice(first, first + width)
            nc.vector.quantize_mx(out=ds_mx[g][0][:, cols].bitcast(E5M2), scales=ds_mx[g][1][:, cols], in_=grouped[:].rearrange("p n t -> p (n t)"))

        def quantize_qm(g, j):
            later = j // 2
            if later not in qm_mx:
                width = 2 * PASSES * P
                qm_mx[later] = (keep.tile([P, width], U32, name="qm_codes%d" % later, align_bytes=64),
                                keep.tile([P, width], U8, name="qm_scales%d" % later, tag="qm_scales%d" % later, align_bytes=64), E4M3)
            place = j % 2 * PASSES + g
            cols = slice(place * P, (place + 1) * P)
            nc.vector.quantize_mx(out=qm_mx[later][0][:, cols].bitcast(E4M3), scales=qm_mx[later][1][:, cols],
                                  in_=qm_dealt[g, j // 2][:, j % 2, :, :].rearrange("p s j -> p (s j)"))

        last_widths = (N // 2, N // 4, N // 4)
        last_firsts = (0, N // 2, 3 * N // 4)
        prepare_do(0)
        prepare_do(1)
        form_ds(0, (N // 2, N // 2), [(i, t) for i in range(2) for t in range(PACK)])
        form_ds(1, last_widths, [(i, t) for i in range(3) for t in range(PACK)])
        first_parts = [regroup_ds("ds_grouped0%d" % h, "SG"[h], ds_flat[0, h][:], N // 2, "do1%d" % h) for h in range(2)]
        qm_dealt = {}
        qm_dealt[0, 0] = deal("S", "qm00", qm_raw[0][:], 0)
        first_half = keep.tile([P, N // 2, PACK], BF16, name="ds_grouped10", align_bytes=64)
        nc.gpsimd.tensor_scalar(out=first_half[:, :P, :], in0=ds_flat[1, 0][:, :, :P].rearrange("p t n -> p n t"),
                                scalar1=1.0, scalar2=0.0, op0=ALU.mult, op1=ALU.add)
        move("S", first_half[:, P:, :].rearrange("p (c i) t -> p c t i", i=4), ds_flat[1, 0][:, :, P:].rearrange("p t (c i) -> p c t i", i=4))
        last_parts = [first_half] + [regroup_ds("ds_grouped1%d" % i, "S", ds_flat[1, i][:], last_widths[i], "ds_grouped1%d" % i) for i in (1, 2)]
        for h in range(2):
            quantize_ds(0, h * N // 2, N // 2, first_parts[h])
        for j in range(2):
            quantize_qm(0, j)
        quantize_ds(1, last_firsts[0], last_widths[0], last_parts[0])
        dealt_row = keep.tile([P, 3 * K_PASS], BF16, name="dealt_row", align_bytes=64)
        qm_dealt[1, 0] = dealt_row[:, K_PASS:].rearrange("p (u s j) -> p u s j", u=2, j=PACK)
        for engine, rows in (("V", slice(0, P // 2)), ("S", slice(P // 2, P))):
            move(engine, qm_dealt[1, 0][:, :, rows, :].rearrange("p u s j -> p s j u"),
                 qm_raw[1][:].rearrange("p j (s c) -> p s j c", c=PACK)[:, rows, :, 0:2])
        for i in (1, 2):
            quantize_ds(1, last_firsts[i], last_widths[i], last_parts[i])
        for j in range(2):
            quantize_qm(1, j)
        qm_dealt[0, 1] = dealt_row[:, :2 * K_PASS].rearrange("p (u s j) -> p u s j", u=2, j=PACK)
        move("V", qm_dealt[0, 1].rearrange("p u s j -> p s j u"), qm_raw[0][:].rearrange("p j (s c) -> p s j c", c=PACK)[:, :, :, 2:4])
        qm_dealt[1, 1] = keep.tile([P, 2, P, PACK], BF16, name="qm11_dealt", tag="ds_flat12", align_bytes=64)
        for engine, rows in (("S", slice(0, 3 * P // 4)), ("V", slice(3 * P // 4, P))):
            move(engine, qm_dealt[1, 1][:, :, rows, :].rearrange("p u s j -> p s j u"),
                 qm_raw[1][:].rearrange("p j (s c) -> p s j c", c=PACK)[:, rows, :, 2:4])

        out_rows = out_0.rearrange("(p j) c -> p j c", j=PACK)
        flat = []
        for half in range(2):
            flat.append(keep.tile([P, 2, T // 2, 2], BF16, name="flat%d" % half, tag=("v0", "ds1_codes")[half], align_bytes=64))

        def round_plane(engine, j, first, width):
            half, at = divmod(first, T // 2)
            move(engine, flat[half][:, j // 2, at:at + width, j % 2], windows[j][:, first:first + width])

        dk = [None] + [bank("dk", 0, j) for j in range(1, PACK)]
        dk_halves = [psum.tile([P, N // 2], F32, name="dk_half%d" % h, tag=("bank00", "bank12")[h]) for h in range(2)]
        for h in range(2):
            product(dk_halves[h][:], qm_mx[0], 0, ds_mx[0], True, False, slice(h * N // 2, (h + 1) * N // 2))
        for i in range(3):
            h, at = divmod(last_firsts[i], N // 2)
            product(dk_halves[h][:, at:at + last_widths[i]], qm_mx[0], 1, ds_mx[1], False, i != 1,
                    slice(last_firsts[i], last_firsts[i] + last_widths[i]))
        for j in range(PACK):
            dk_sb = keep.tile([P, N], F32, name="dk_sb%d" % j, tag=("k0", "do_raw01", "v1", "do_raw00")[j], align_bytes=64)
            if j == 0:
                for h in range(2):
                    move("S", dk_sb[:, h * N // 2:(h + 1) * N // 2], dk_halves[h][:])
            else:
                move("S", dk_sb[:], dk[j][:])
            if SCAT[j] == "V":
                nc.vector.tensor_copy(out=windows[j][:].indirect(offsets[:]), in_=dk_sb[:])
            else:
                for h in range(2):
                    nc.scalar.activation(out=windows[j][:].indirect(offsets[:, h * N // 32:(h + 1) * N // 32]),
                                         in_=dk_sb[:, h * N // 2:(h + 1) * N // 2], func=ACT.Copy)
            nc.sync.dma_start(out=out_rows[:, j, :], in_=windows[j][:])
            if j == 0:
                for u in range(2):
                    for g in range(PASSES):
                        quantize_qm(g, 2 + u)
                for jj in range(1, PACK):
                    for g in range(PASSES):
                        product(dk[jj][:], qm_mx[jj // 2], jj % 2 * PASSES + g, ds_mx[g], g == 0, g == PASSES - 1)
        for engine, j, first, width in ROUND:
            round_plane(engine, j, first, width)

        out_codes = keep.tile([P, T], U32, name="out_codes", tag="k3", align_bytes=64)
        out_scales = keep.tile([P, CW], U8, name="out_scales", align_bytes=64)
        words = out_1[0].rearrange("p c l -> p (c l)").bitcast(I32)
        scale_rows = out_2[0].bitcast(I32)

        def store_scales(queues):
            for quad in range(4):
                queues[quad].dma_start(out=scale_rows[4 * quad:4 * quad + 4, :].rearrange("f (c w) -> c f w", c=CHUNKS),
                                       in_=out_scales[32 * quad:32 * quad + 4 * CHUNKS, :].bitcast(I32))

        grouped_out = {}
        for c in (2, 3, 0, 1):
            grouped_out[c] = keep.tile([P, CW, PACK], BF16, name="grouped_out%d" % c, tag=("k_grouped", "v_grouped", "v2", "v3")[c], align_bytes=64)

        def interleave(engine, c, first, width):
            at = (c % 2) * CW + first
            word = I32 if engine == "V" else U32
            pairs = flat[c // 2][:].rearrange("p q n e -> p q (n e)").bitcast(word)
            move(engine, grouped_out[c][:].bitcast(word)[:, first:first + width, :].rearrange("p (c i) q -> p c q i", i=4),
                 pairs[:, :, at:at + width].rearrange("p q (c i) -> p c q i", i=4))

        def quantize_chunk(c, first, width):
            cols = slice(c * CW + first, c * CW + first + width)
            nc.vector.quantize_mx(out=out_codes[:, cols].bitcast(E4M3), scales=out_scales[4 * c:P, first:first + width],
                                  in_=grouped_out[c][:, first:first + width, :].rearrange("p n j -> p (n j)"))

        def store_words(first, width):
            cols = slice(first, first + width)
            nc.sync.dma_start(out=words[:, cols], in_=out_codes[:, cols].bitcast(I32))

        for engine, c, first, width in EARLY:
            interleave(engine, c, first, width)
        for chunks in ((2,), (0,), (1,), (3,)):
            for c in chunks:
                for first in (0, CW // 2):
                    quantize_chunk(c, first, CW // 2)
            store_words(chunks[0] * CW, len(chunks) * CW)
        store_scales((nc.scalar, nc.scalar, nc.scalar, nc.scalar))
